import numpy as np, ml_dtypes
CORES = [66,74,82,90,194,202,210,218]
N = 8
import mx_ref
BF = ml_dtypes.bfloat16
def gcols(t, e):
    v = np.concatenate([t.reshape(8, 16, -1, 4), np.zeros((8, 16, 1, 4), BF)], axis=2)
    return np.ascontiguousarray(np.stack([v[g][:, e[g]] for g in range(8)])).reshape(128, -1)
def tile(rs):
    return np.stack(rs, axis=2).reshape(128, -1).astype(BF)
def pick(q, e):
    c = np.concatenate([q[0].reshape(128, -1, 4), np.zeros((128, 1, 4), np.uint8)], axis=1); s = np.concatenate([q[1], np.ones((16, 1), np.uint8)], axis=1)
    return (np.ascontiguousarray(c[:, e].reshape(128, -1)), np.ascontiguousarray(s[:, e]))
def join(*qs):
    return (np.concatenate([q[0] for q in qs], axis=1), np.concatenate([q[1] for q in qs], axis=1))
def put(q, e, v):
    c, s = q[0].reshape(128, -1, 4).copy(), q[1].copy(); c[:, e] = v[0].reshape(128, -1, 4); s[:, e] = v[1]
    return (c.reshape(128, -1), s)
def pk(c, s):
    return (np.ascontiguousarray(c), mx_ref.live(s))
def emit(q):
    return q[0], q[1]
def packed(v, rng):
    q = [mx_ref.quantize(np.ascontiguousarray(v[r])) for r in range(N)]
    return np.stack([a for a, b in q]), np.stack([mx_ref.plane(b, rng) for a, b in q])
def values_of_codes():
    e, c = np.zeros((128, 128, 4), np.float32), np.zeros((128, 2, 4), np.uint8)
    e[np.arange(128), np.arange(128), 0] = 1
    c[:127, :, 0] = np.arange(256).reshape(2, 128).T[:127]
    return mx_ref.matmul(mx_ref.quantize(e.reshape(128, 512).astype(BF)), (c.reshape(128, 8), np.full((16, 2), 127, np.uint8))).T.reshape(-1).astype(np.float64)
CODE_VALUE, SCALE_VALUE = values_of_codes(), 2.0 ** (np.arange(256) - 127.0)
def decode(q):
    return (CODE_VALUE[q[0]].reshape(16, 8, -1, 4) * SCALE_VALUE[q[1]][:, None, :, None] + 0.0).reshape(128, -1).astype(np.float32)
def f(rng, *shape):
    return mx_ref.flush((rng.standard_normal(shape, dtype=np.float32) * np.exp2(rng.integers(-2, 3, shape[:-1] + (1,)))).astype(BF))
def wide(rng, *shape, cols=0):
    v = rng.standard_normal(shape, dtype=np.float32) * np.exp2(rng.integers(-12, 13, shape)).astype(np.float32)
    if cols: v *= np.repeat(np.exp2(rng.integers(-cols, cols + 1, shape[:-2] + (1, shape[-1] // 4))) * (rng.random(shape[:-2] + (1, shape[-1] // 4)) > 0.0625), 4, axis=-1).astype(np.float32)
    return mx_ref.flush(v.astype(BF))
C, R = 288, 2
def alike(w):
    return np.stack([w] * N)
def layers(rng):
    return f(rng, N, 128, 4096)
def weights(rng, w, still=()):
    w = np.array(w).reshape(N, 8, 16, 8, 8, 16, 4)
    for i in still:
        w[:, :, i] = 0
        w[:, :, :, :, :, i] = 0
    c, p = packed(w.reshape(N, 128, 4096), rng)
    return {"wc": c, "ws": p}
def numbers_of(rng):
    return {"x": np.array(f(rng, N, 128, 4 * C)), "u": alike(f(rng, 128, 512)), "v": np.array(f(rng, N, 128, 512))}
def unscored(rng):
    a = np.array(f(rng, 128, 512)).reshape(128, 128, 4)
    a[:, ::16] = 0
    a[:, 1::16] = 0
    return a
def setup_inputs(rng):
    return {**numbers_of(rng), **weights(rng, layers(rng))}
def setup_inputs_ties(rng):
    d = numbers_of(rng)
    o = rng.permutation(N)
    k = rng.integers(0, 3, (N, 8, C))
    m = np.where((o % 2 == 0)[:, None, None], k, rng.integers(-2, 3, (N, 8, C)))
    k[o == 0] = 0
    m[o == 0] = 0
    k[o == 1] *= -1
    x = d["x"].reshape(N, 8, 16, C, 4)
    x[:, :, 0] = 0
    x[:, :, 0, :, 0] = k.astype(np.float32).astype(BF)
    x[:, :, 0, :, 1] = m.astype(np.float32).astype(BF)
    a = unscored(rng)
    for h in range(0, 128, 16):
        a[h, h, 0] = 1
        a[h, h + 1, 1] = 1
    return {"x": x.reshape(N, 128, 4 * C), "u": alike(a.reshape(128, 512)), "v": d["v"], **weights(rng, layers(rng), [0])}
def setup_inputs_near(rng):
    d = numbers_of(rng)
    x = d["x"].astype(np.float32).reshape(N, 8, 16, C, 4)
    x[:, :, 0] = 0
    x[:, :, 8:] = 0
    a = unscored(rng)
    o = rng.permutation(8) % 4
    for g in range(8):
        h = 16 * g
        for m in range(2):
            s = rng.integers(0, 16, (N, C))
            c = rng.integers(0, 2, (N, C)) * 2.0 - 1.0
            if o[g] < 3: x[:, g, 8 + m] = ((s[:, :, None] >> np.arange(4)) & 1) * np.exp2(np.arange(4) - 23.0)
            if o[g] < 2:
                k = 1.0 if o[g] == 0 else 2.0 ** -30
                x[:, g, 0, :, m] = c
                x[:, g, 11, :, 0] = 2.0 ** -10
                a[h, h + m, m] = k
                a[h + 8 + m, h + m] = k
                a[h + 11, h + m, 0] = k
            elif o[g] == 2:
                for r in range(N): x[r, g, 0, rng.permutation(C)[:2], m] = [1.0, -1.0]
                a[h, h + m, m] = 2.0 ** 30
                a[h + 8 + m, h + m] = 2.0 ** -30
            else:
                x[:, g, 10, :, m] = np.where(s % 2 == 0, 1.125 * 2.0 ** -30 * c, 0.0)
                x[:, g, 12, :, m] = np.where(s % 2 == 0, 0.0, 1.25 * 2.0 ** -30 * c)
                a[h + 10, h + m, m] = 1.125 * 2.0 ** -30
                a[h + 12, h + m, m] = 2.0 ** -30
    return {"x": x.reshape(N, 128, 4 * C).astype(BF), "u": alike(a.reshape(128, 512)), "v": d["v"], **weights(rng, layers(rng), [0, 8, 9, 10, 11, 12, 13, 14, 15])}
def setup_inputs_odd(rng):
    d = numbers_of(rng)
    a = (1.0 + (2 * rng.integers(0, 64, (N, 16, 8, C, 4)) + 1) * 2.0 ** -7) * np.exp2(-rng.integers(8, 15, (N, 16, 8, C, 4)).astype(np.float64))
    a = np.where(np.arange(8)[:, None, None] * 4 + np.arange(4) == rng.integers(0, 32, (N, 16, 1, C, 1)), 1.96875, a)
    a = a * (rng.integers(0, 2, a.shape) * 2.0 - 1.0) * np.exp2(rng.integers(-2, 3, (N, 16, 1, C, 1)).astype(np.float64))
    return {"x": a.astype(np.float32).reshape(N, 128, 4 * C).astype(BF), "u": d["u"], "v": d["v"], **weights(rng, layers(rng), [8, 9, 10, 11, 12, 13, 14, 15])}
def setup_inputs_ends(rng):
    d = numbers_of(rng)
    o = rng.permutation(N) % 4
    x = np.zeros((N, 8, 16, C, 4), np.float32)
    x[:, :, 8:12] = f(rng, N, 8, 4, C, 4).astype(np.float32) * np.float32(1024)
    for r in range(N):
        c = rng.integers(0, 2, C) * 2.0 - 1.0
        w = rng.choice([1.375, 1.5], (8, C))
        a, b = rng.permutation(C)[:2]
        w[:, b] = 1.625
        if o[r] == 0:
            w[:, a] = 1.625
            c[a], c[b] = 1.0, -1.0
        else: w[:, a] = 1.25
        if o[r] == 1: c[:] = -1.0
        if o[r] == 2: c[:] = 1.0
        e = w * c * 2.0 ** 29 if o[r] < 2 else np.ones((8, 1)) * c * 2.0 ** -30
        x[r, :, :8] = e[:, None, :, None]
        k = (rng.integers(0, 2, (128, 512)) * 2.0 - 1.0).astype(np.float32)
        if o[r] == 1: d["v"][r] = (k * np.float32(2.0 ** 30)).astype(BF)
        if o[r] == 2: d["v"][r] = (k * np.float32(2.0 ** -30)).astype(BF)
    u = unscored(rng).reshape(8, 16, 128, 4)
    p = rng.permutation(8)
    for g in range(8):
        k = (2.0 ** 30 if p[g] < 4 else 2.0 ** -29) * (1.0 if p[g] % 2 == 0 else -1.0)
        for m in range(2):
            u[:, :8, 16 * g + m] = 0.75 * k * (1 - 2 * m)
            u[g, :8, 16 * g + m] = k * (1 - 2 * m)
    w = ((rng.integers(0, 2, (N, 128, 4096)) * 2.0 - 1.0) * 2.0 ** -11).astype(np.float32).astype(BF)
    return {"x": x.reshape(N, 128, 4 * C).astype(BF), "u": alike(u.reshape(128, 512)), "v": d["v"], **weights(rng, w, [0, 1, 2, 3, 4, 5, 6, 7])}
def setup_inputs_spread(rng):
    d = numbers_of(rng)
    w = np.array(mx_ref.flush((layers(rng).astype(np.float32) * np.float32(2.0 ** -7)).astype(BF)))
    x = np.array(wide(rng, N, 128, 4 * C, cols=3))
    e = int(rng.integers(N))
    x[e] = ((1.0 + 0.25 * rng.random((128, 4 * C))) * 2.0 ** 24).astype(np.float32).astype(BF)
    w[e ^ 1] = (-0.1875 - 0.0625 * rng.random((128, 4096))).astype(np.float32).astype(BF)
    return {"x": x, "u": d["u"], "v": d["v"], **weights(rng, w)}
def check_inputs(d):
    b = []
    for k in ("x", "u", "v"):
        a = np.abs(d[k].astype(np.float32))
        if not (np.isfinite(a).all() and ((a == 0) | (a >= 2.0 ** -30) & (a <= 2.0 ** 30)).all()): b.append("a value of " + k)
    if (d["u"] != d["u"][:1]).any(): b.append("u isn't the same on all ranks")
    none, least, most = [emit(mx_ref.quantize(np.full((128, 16), k, np.float32).astype(BF)))[1][0, 0] for k in (0.0, 2.0 ** -30, 2.0 ** 30)]
    size = 0.0
    for r in range(N):
        if ((d["wc"][r] == 0x7F) | (d["wc"][r] == 0xFF)).any(): b.append("wc: a code that is no number")
        s = mx_ref.live(d["ws"][r])
        if ((s != none) & ((s < least) | (s > most))).any(): b.append("ws: a scale out of range")
        if (((d["wc"][r].reshape(16, 8, -1, 4) & 0x7F) != 0) & (s == none)[:, None, :, None]).any(): b.append("wc: a code other than zero where the scale is that of zeros")
        size = max(size, float(np.abs(decode(pk(d["wc"][r], d["ws"][r]))).max()))
    if not float(np.abs(d["x"].astype(np.float32)).max()) * (1.0 + 20.0 * size) * (1.0 + 20.0 * size) <= 900000000.0: b.append("the sizes of x and W together")
    return b
def places(s):
    o = np.argsort(-s, axis=1, kind="stable")
    i = np.zeros(s.shape, np.int64)
    np.put_along_axis(i, o, np.broadcast_to(np.arange(C), s.shape), axis=1)
    return o, i
def reference(x, u, v, wc, ws):
    qu = [mx_ref.quantize(u[r]) for r in range(N)]
    lay = [pk(wc[r], ws[r]) for r in range(N)]
    now = [x[r] for r in range(N)]
    total = np.zeros((N, C), np.int64)
    for t in range(R):
        q = [mx_ref.quantize(now[r]) for r in range(N)]
        full = [decode(q[r]).astype(BF) for r in range(N)]
        s = [mx_ref.matmul(qu[r], q[r]) + np.float32(0.0) for r in range(N)]
        first = [places(s[r][::16]) for r in range(N)]
        second = [places(s[r][1::16])[1] for r in range(N)]
        made = [None] * N
        for r in range(N):
            e = r ^ (1 << t)
            total[r] = first[r][1][0]
            took = np.zeros((8, C), np.int64)
            for g in range(8):
                turn = places(total[r][None])[1][0]
                took[g] = first[e][0][g][turn]
                total[r] = total[r] + second[e][g][took[g]]
            z = mx_ref.quantize(gcols(full[e], took))
            p = [mx_ref.matmul(pick(lay[r], np.arange(128 * b, 128 * b + 128)), z) for b in range(8)]
            y = tile([np.maximum(p[b], p[b + 4]) * np.float32(0.03125) for b in range(4)])
            back = gcols(decode(mx_ref.quantize(y)).astype(BF), np.argsort(took, axis=1))
            made[e] = (full[e].astype(np.float32) + back.astype(np.float32)).astype(BF)
        now = made
    y, tot = np.zeros((N, 128, C), np.float32), np.zeros((N, 1, C), np.float32)
    oc, osc = np.zeros((N, 128, 4 * C), np.uint8), np.zeros((N, 16, C), np.uint8)
    for r in range(N):
        q = mx_ref.quantize(now[r])
        y[r] = mx_ref.matmul(mx_ref.quantize(v[r]), q)
        tot[r, 0] = total[r]
        oc[r], osc[r] = emit(q)
    return {"y": y, "tot": tot, "oc": oc, "osc": osc}

@@ -1,0 +1,445 @@
+from concourse.mybir import dt, AluOpType as A, ActivationFunctionType as F
+
+C = 288
+H = C // 2
+KW = 512
+B16, B96 = 2.0 ** 18, 2.0 ** 21
+BIG, TINY, MAGIC = 1e29, 2.0 ** -119, 1.5 * 2.0 ** 23
+NK = 17
+
+MXC, PL = "float8_e4m3fn_x4", "uint8"
+SCRATCH = {}
+
+
+def _buf(n, cols, d):
+    SCRATCH[n] = ("psum" if n == "ps" else "sbuf", [128, cols], d)
+
+
+_buf("ps", 4096, "float32")
+for _t in range(3):
+    _buf("xt%d" % _t, 4 * C, "bfloat16")
+    _buf("xc%d" % _t, C, MXC)
+    _buf("xs%d" % _t, C, PL)
+for _t in range(2):
+    for _n in ("l", "z", "q", "b"):
+        _buf(_n + "c%d" % _t, C, MXC)
+        _buf(_n + "s%d" % _t, C, PL)
+for _n, _c, _d in (("wk", 1024, MXC), ("wp", 1024, PL), ("ut", 512, "bfloat16"), ("vt", 512, "bfloat16"), ("uq", 128, MXC), ("us", 128, PL),
+                   ("vq", 128, MXC), ("vs", 128, PL), ("up", 640, MXC), ("ups", 640, PL), ("kt", NK * 512, "bfloat16"), ("kc", NK * 128, MXC),
+                   ("ks", NK * 128, PL), ("tm2", 512, "bfloat16"), ("ui", 40, "int32"), ("ul", 40, "uint16"), ("pi", 2, "int32"), ("pj", 4, "int32"),
+                   ("fc", 16, "float32"), ("gm", 8, "float32"), ("bcm", 8, "float32"), ("ij", C, "float32"), ("rowx", C, "float32"),
+                   ("row16", C, "float32"), ("row32", C, "float32"), ("row96", C, "float32"), ("rowog", 128, "float32"), ("hown", C, "float32"),
+                   ("hb", C, "float32"), ("k16", C, "float32"), ("k96", C, "float32"), ("t1", C, "float32"), ("t2", C, "float32"),
+                   ("t3", C, "float32"), ("t4", C, "float32"), ("wo", 4 * C, "bfloat16"), ("qo", C, MXC), ("qos", C, PL), ("om", C, "float32"),
+                   ("wa", 20 * C, "bfloat16"), ("wb", 20 * C, "bfloat16"), ("qa", 5 * C, MXC), ("qas", 5 * C, PL), ("qb", 5 * C, MXC),
+                   ("qbs", 5 * C, PL), ("rm", 4 * C, "float32"), ("tr", 4 * C, "float32"), ("ds", 6 * C, "float32"), ("dd", C, "float32"),
+                   ("key0", C, "float32"), ("key1", C, "float32"), ("col", C, "float32"), ("cb", 2, "float32"), ("nl", 18, "uint16"),
+                   ("nf", 18, "float32"), ("na", 18, "float32"), ("nz", 18, "uint16"), ("aw", 18, "uint16"), ("ow", 18, "uint16"),
+                   ("kw", 18, "uint16"), ("bs", C, "float32"), ("cs", C, "float32"), ("of", C, "float32"), ("nv", C, "float32"),
+                   ("kr", C, "float32"), ("cd", 4 * C, "bfloat16"), ("qc", C, MXC), ("qcs", C, PL), ("cw", 8 * C, "float32"),
+                   ("ct", 4 * C, "bfloat16"), ("qt", C, MXC), ("qts", C, PL), ("ff", 4 * C, "bfloat16"), ("fs", 4 * C, "bfloat16"),
+                   ("zt", 4 * C, "bfloat16"), ("y1", 4 * C, "float32"), ("ym", 4 * C, "bfloat16"), ("yt", 4 * C, "bfloat16"),
+                   ("yo", C, "float32"), ("to", C, "float32")):
+    _buf(_n, _c, _d)
+DMAS = ["d%d" % i for i in range(20)]
+SEMAPHORES = ["cv", "cs", "ct", "cg", "sent", "ax0", "ax1", "ay0", "ay1"] + DMAS
+
+
+def rank_program(g, core, T, topo):
+    rank = T.rank_of(core)
+    if rank is None:
+        return
+    Q = {"g": g, "v": g.vector, "s": g.scalar, "t": g.tensor, "y": g.sync}
+    clk = {k: {} for k in Q}
+    cnt = {k: 0 for k in Q}
+    last, readers, ndma, sent = {}, {}, [0], [0]
+
+    def waits(q, toks):
+        for s, v, c, _ in sorted(toks, key=lambda k: -len(k[2])):
+            if clk[q].get(s, 0) < v:
+                Q[q].wait_ge(T.sem[s], max(k[1] for k in toks if k[0] == s))
+                for k in toks:
+                    if k[0] == s:
+                        for a, b in k[2].items():
+                            if clk[q].get(a, 0) < b: clk[q][a] = b
+
+    def op(q, fn, rd=(), wr=(), dma=False):
+        rd = (rd,) if isinstance(rd, str) else rd
+        wr = (wr,) if isinstance(wr, str) else wr
+        me = "dma" if dma else q
+        toks = []
+        for k in rd:
+            if k in last: toks.append(last[k])
+            if k[:2] == "ps": toks += [w for w in readers.get(k, {}).values() if w[3] != me]
+        for k in wr:
+            if k in last and not (q == "t" and last[k][3] == "t"): toks.append(last[k])
+            toks += [w for w in readers.get(k, {}).values() if w[3] != me or dma]
+        waits(q, toks)
+        ins = fn()
+        if dma:
+            s, v = DMAS[ndma[0]], 16
+            ndma[0] += 1
+        else:
+            cnt[q] += 1
+            s, v = "c" + q, cnt[q]
+        ins.then_inc(T.sem[s], 16 if dma else 1)
+        c = dict(clk[q])
+        c[s] = v
+        tok = (s, v, c, me)
+        for k in rd:
+            readers.setdefault(k, {})[s] = tok
+        for k in wr:
+            last[k] = tok
+            readers[k] = {}
+
+    V, S = g.vector, g.scalar
+
+    def ts(out, i, s1, s2, o0, o1, rd, wr):
+        if o1 is None: op("v", lambda: V.tensor_scalar(out, i, s1, None, o0), rd, wr)
+        else: op("v", lambda: V.tensor_scalar(out, i, s1, s2, o0, o1), rd, wr)
+
+    def tt(out, a, b, o, rd, wr):
+        op("v", lambda: V.tensor_tensor(out, a, b, o), rd, wr)
+
+    def cp(out, i, rd, wr):
+        op("v", lambda: V.tensor_copy(out, i), rd, wr)
+
+    def ms(ap, c, wr):
+        op("v", lambda: V.memset(ap, c), (), wr)
+
+    def act(out, i, f, rd, wr, bias=0.0, scale=1.0):
+        op("s", lambda: S.activation(out, i, f, bias=bias, scale=scale), rd, wr)
+
+    def qz(c, s, i, rd, wr):
+        op("v", lambda: V.quantize_mx(c, s, i), rd, wr)
+
+    def iota(out, pat, base, cm, wr, flag=True):
+        op("g", lambda: g.iota(out, pat, base, cm, allow_small_or_imprecise_dtypes=flag), (), wr)
+
+    def ld(q, out, i, wr, rd=()):
+        op(q, lambda: Q[q].dma_start(out, i), rd, wr, dma=True)
+
+    def ps(b, n=C):
+        return T.ps[:, 512 * b:512 * b + n]
+
+    def mm(b, n, lc, ls, rc, rs, rd, start=True, stop=True):
+        op("t", lambda: g.tensor.matmul_mx(ps(b, n), lc, ls, rc, rs, start, stop), rd, "ps%d" % b)
+
+    def kk(i):
+        return T.kc[:, 128 * i:128 * i + 128], T.ks[:, 128 * i:128 * i + 128]
+
+    def kz(k):
+        qz(*kk(k), T.kt[:, k * KW:(k + 1) * KW], "kt%d" % k, "kc%d" % k)
+
+    def scan(out, i, k, rd, wr):
+        op("v", lambda: V.tensor_tensor_scan(out, i, k, -4.0 * B96, A.max, A.add), rd, wr)
+
+    def send(src, dst, sem, peer):
+        waits("g", [last[k] for k in src])
+        rid, pid = topo.addr(peer, core)
+        m = topo.mask(core, peer)
+        g.remote_dma(T[dst[0]][:].bitcast(dt.uint8), T[src[0]][:].bitcast(dt.uint8), T.sem[sem], T.sem.sent, pid, rid, m)
+        g.remote_dma(T[dst[1]][:], T[src[1]][:], T.sem[sem], T.sem.sent, pid, rid, m)
+        n = 2 * len(topo.engines(core, peer))
+        sent[0] += n
+        for k in dst:
+            last[k] = (sem, n, {sem: n}, "r")
+
+    peers = [T.cores[rank ^ (1 << t)] for t in range(2)]
+
+    ld("y", T.xt0[:], T.x[:], "xt0")
+    ld("s", T.ut[:], T.u[:], "ut")
+    ld("y", T.wk[:].bitcast(dt.uint8), T.wc[:], "wk")
+    ld("y", T.wp[:], T.ws[:], "wp")
+    ld("y", T.vt[:], T.v[:], "vt")
+
+    iota(T.pi[:, 0:1], [[1, 1]], 0, 1, "pi", False)
+    iota(T.ui[:, 0:16], [[16, 2], [32, 4], [0, 2]], 0, 0, "ui", False)
+    iota(T.ui[:, 16:32], [[16, 2], [32, 4], [0, 2]], 1, 0, "ui", False)
+    iota(T.rowx[:, 0:256], [[0, 2], [1, 128]], 0, 0, "rowx")
+    iota(T.rowx[:, 256:C], [[1, 32]], 96, 0, "rowx")
+    iota(T.row16[:], [[0, 18], [1, 16]], 0, 0, "row16")
+    iota(T.rowog[:], [[1, 8], [0, 16]], 0, 0, "rowog")
+    iota(T.ij[:], [[1, C]], 0, 0, "ij")
+
+    def col(i):
+        return T.fc[:, i:i + 1]
+
+    def picker(row, rn, c0, c1, step):
+        for t, n, c in ((T.t1, "t1", c0), (T.t2, "t2", c1)):
+            act(t[:], row, F.Abs, (rn, "f%d" % c), n, bias=col(c))
+            act(t[:], t[:], F.Relu, n, n, bias=T.fc[:, 14:15] if step == B16 else T.fc[:, 15:16], scale=-step)
+
+    ms(T.fc[:, 14:15], B16, "f14")
+    ms(T.fc[:, 15:16], B96, "f15")
+    ms(T.ui[:, 32:40], 0, "uz")
+    cp(col(0), T.pi[:, 0:1], "pi", "f0")
+    for i, (o, k) in enumerate(((A.bitwise_and, 15), (A.bitwise_and, 31), (A.arith_shift_right, 4), (A.arith_shift_right, 5))):
+        ts(T.pj[:, i:i + 1], T.pi[:, 0:1], k, None, o, None, "pi", "pj")
+    cp(T.fc[:, 1:5], T.pj[:], "pj", "f1")
+    for i, j, a, b in ((10, 0, -BIG, -0.5 * BIG), (5, 1, -1.0, 0.0), (6, 1, -1.0, 1.0), (7, 2, BIG, -0.5 * BIG), (8, 0, -1.0, 0.0),
+                       (9, 0, -1.0, 1.0), (11, 4, 2.0, 0.0), (12, 4, 2.0, 1.0)):
+        ts(col(i), col(j), a, b, A.mult, A.add, ("f0", "f1"), "f%d" % i)
+    act(T.hown[:], T.rowx[:], F.Identity, ("rowx", "f10"), "hown", bias=col(10), scale=BIG)
+    picker(T.row16[:], "row16", 5, 6, B16)
+    for w, (lo, hi, val) in ((0, (0, 128, 512.0)), (1, (0, 128, 512.0)), (3, (0, 128, -512.0)), (2, (0, 128, 0.0)), (2, (96, 128, 512.0))):
+        ms(T.kt[lo:hi, 7 * KW + w:8 * KW:4], val, "kt7")
+    cp(T.ul[:], T.ui[:], ("ui", "uz"), "ul")
+    for k in (8, 0, 1, 2, 3):
+        ms(T.kt[:, k * KW:(k + 1) * KW], 0.0, "kt%d" % k)
+    qz(T.uq[:], T.us[:], T.ut[:], "ut", ("uq", "us"))
+
+    def upick(i):
+        a, b = 128 * i, 128 * i + 128
+        off = T.ul[:, 8 * i:8 * i + 8]
+        op("v", lambda: V.tensor_copy(T.up[:, a:b].bitcast(dt.uint32), T.uq[:, 0:128].bitcast(dt.uint32).indirect(off)), ("uq", "ul"), "up%d" % i)
+        op("s", lambda: S.activation(T.ups[:, a:b], T.us[:, 0:128].indirect(off), F.Copy), ("us", "ul"), "ups%d" % i)
+
+    upick(4)
+    qz(T.xc0[:], T.xs0[:], T.xt0[:], "xt0", ("xc0", "xs0"))
+    send(("xc0", "xs0"), ("lc0", "ls0"), "ax0", peers[0])
+    iota(T.row32[:], [[0, 9], [1, 32]], 0, 0, "row32")
+    iota(T.row96[:], [[0, 3], [1, 96]], 0, 0, "row96")
+    kz(7)
+    tt(T.k16[:], T.t1[:], T.t2[:], A.subtract, ("t1", "t2"), "k16")
+    ts(T.k16[:, 15:C:16], T.k16[:, 15:C:16], -2.0 * B16, None, A.add, None, "k16", "k16")
+    ts(T.t3[:, 0:128], T.rowog[:], col(11), None, A.is_equal, None, ("rowog", "f11"), "t3")
+    ts(T.t4[:, 0:128], T.rowog[:], col(12), None, A.is_equal, None, ("rowog", "f12"), "t4")
+    for i in range(4):
+        upick(i)
+    for k, w in ((4, (1.0, 1.0)), (5, (0.5, 0.5)), (6, (0.5, -1.0))):
+        for t in range(4):
+            src, n = (T.t3, "t3") if t < 2 else (T.t4, "t4")
+            act(T.kt[:, k * KW + t:(k + 1) * KW:4], src[:, 0:128], F.Copy, n, "kt%d" % k, scale=w[t % 2])
+    act(T.hb[:], T.row32[:], F.Identity, ("row32", "f7"), "hb", bias=col(7), scale=-BIG)
+
+    def early_spread(ks):
+        for k in ks:
+            act(T.kt[:, (9 + k) * KW:(10 + k) * KW], T.tm2[:], F.Copy, ("tm2", "bcm"), "kt%d" % (9 + k), scale=T.bcm[:, k:k + 1])
+
+    def late_constants():
+        ts(T.gm[:], T.ij[:, 0:8], col(3), None, A.is_equal, None, ("ij", "f1"), "gm")
+        ts(T.bcm[:], T.ij[:, 0:8], 16.0, col(0), A.mult, A.is_equal, ("ij", "f0"), "bcm")
+        for t in range(4):
+            ms(T.tm2[:, t:512:4], 8192.0 if t < 2 else 0.0, "tm2")
+        for t, w in enumerate((1.0, 1.0, 0.5)):
+            ms(T.kt[0:96, 8 * KW + t:9 * KW:4], w, "kt8")
+        for t in range(2, 4):
+            ms(T.cd[:, t:4 * C:4], 0.0, "cdz")
+        ms(T.ct[:, 3:4 * C:4], 0.0, "ctz")
+        picker(T.row96[:], "row96", 8, 9, B96)
+        early_spread((0, 1))
+        for k in (4, 5, 6):
+            kz(k)
+
+    def last_constants():
+        for i in (9, 10, 8):
+            kz(i)
+        tt(T.k96[:], T.t1[:], T.t2[:], A.subtract, ("t1", "t2"), "k96")
+        ts(T.k96[:, 95:C:96], T.k96[:, 95:C:96], -2.0 * B96, None, A.add, None, "k96", "k96")
+
+    dv = T.dd[:, 15:C:16]
+    wo, ct = T.wo, T.ct
+    for t in range(2):
+        peer = peers[t]
+        xc, xs = T["xc%d" % t], T["xs%d" % t]
+        xn = ("xc%d" % t, "xs%d" % t)
+        lc, ls = T["lc%d" % t], T["ls%d" % t]
+        ln = ("lc%d" % t, "ls%d" % t)
+        m0 = (0, 128, 160)
+        mm(3, C, T.up[:, 512:640], T.ups[:, 512:640], xc[:], xs[:], xn + ("up4", "ups4"))
+        for q in range(3):
+            mm(q, 128, xc[:, m0[q]:m0[q] + 128], xs[:, m0[q]:m0[q] + 128], T.uq[:], T.us[:], xn + ("uq", "us"))
+        tt(T.om[:], ps(3), T.hown[:], A.max, ("ps3", "hown"), "om")
+        for q in range(3):
+            sc = T.ps[:, 512 * q:512 * q + 1]
+            rq = ("ps3", "ps%d" % q)
+            e0, e1 = 128 * q, min(128 * q + 128, C)
+            if e0: ts(wo[:, q:4 * e0:4], ps(3, e0), sc, None, A.is_lt, None, rq, "wo")
+            ts(wo[:, 4 * e0 + q:4 * C:4], T.ps[:, 1536 + e0:1536 + C], sc, None, A.is_le, None, rq, "wo")
+            ts(wo[:, 4 * e0 + 3:4 * e1:4], T.om[:, e0:e1], sc, None, A.is_equal, None, ("om", rq[1]), "wo")
+        qz(T.qo[:], T.qos[:], wo[:], "wo", "qo")
+        mm(4, C, *kk(7), T.qo[:], T.qos[:], ("qo", "kc7"))
+        if t == 0:
+            late_constants()
+        scan(T.dd[:], ps(4), T.k16[:], ("ps4", "k16"), "dd")
+        tt(T.key0[:], ps(4), T.ij[:], A.subtract, ("ps4", "ij"), "key0")
+        ts(T.nl[:], dv, -1.0 / 512, 287.0 - B16 / 512, A.mult, A.add, "dd", "nl")
+        ts(T.nf[:], dv, -1.0 / 512, 287.0 - B16 / 512, A.mult, A.add, "dd", "nf")
+        ts(T.na[:], T.nf[:], T.gm[:, 0:1], None, A.mult, None, ("nf", "gm"), "na")
+        banks = ((5, 7), (6, 0), (1, 3), (2, 4))
+        for k in range(4):
+            for b in banks[k]:
+                mm(b, C, T.up[:, 128 * k:128 * k + 128], T.ups[:, 128 * k:128 * k + 128], lc[:], ls[:], ln + ("up%d" % k, "ups%d" % k))
+        for ty in range(2):
+            wt, qn, pb = (T.wa, "qa", 5) if ty == 0 else (T.wb, "qb", 1)
+            qc, qs = T[qn], T[qn + "s"]
+
+            def pl(w, p):
+                return "w%s%d.%d" % (qn, w, p)
+
+            def word(w):
+                c = (4, 4, 4, 5, 6)[w]
+                qz(qc[:, C * w:C * w + C], qs[:, C * w:C * w + C], wt[:, 4 * C * w:4 * C * w + 4 * C], [pl(w, p) for p in range(4)], qn + "%d" % w)
+                mm(pb, C, *kk(c), qc[:, C * w:C * w + C], qs[:, C * w:C * w + C], (qn + "%d" % w, "kc%d" % c), w == 0, w == 4)
+
+            for par in range(2):
+                k = 2 * ty + par
+                bv, bw = banks[k]
+                rv, trn, o = "ps%d" % bv, "tr%d" % k, C * k
+                tt(T.rm[:, o:o + C], ps(bv), T.hb[:], A.max, (rv, "hb"), "rm%d" % k)
+                op("v", lambda: V.transpose(T.tr[:, o:o + C], T.rm[:, o:o + C]), "rm%d" % k, trn)
+                for i, (b, w, p) in enumerate(((0, 3, 0), (1, 3, 1), (8, 4, 0))):
+                    d0 = C * (3 * par + i)
+                    dn = "ds%d" % (3 * par + i)
+                    act(T.ds[:, d0:d0 + C], ps(bw), F.Identity, ("ps%d" % bw, trn), dn, bias=T.tr[:, o + 32 * b:o + 32 * b + 1], scale=-1.0)
+                    z = 4 * C * w + 2 * par + p
+                    if b: act(wt[:, z:z + 128 * b - 3:4], T.ds[:, d0:d0 + 32 * b], F.Sign, (dn, "tny"), pl(w, 2 * par + p), bias=-TINY)
+                    act(wt[:, z + 128 * b:4 * C * (w + 1):4], T.ds[:, d0 + 32 * b:d0 + C], F.Sign, (dn, "tny"), pl(w, 2 * par + p), bias=TINY)
+                tt(wt[:, 16 * C + 2 * par + 1:20 * C:4], ps(bv), T.tr[:, o:o + C], A.is_equal, (rv, trn), pl(4, 2 * par + 1))
+                for b in range(2, 8):
+                    w, p = (b - 2) // 2, 2 * par + b % 2
+                    sc = T.tr[:, o + 32 * b:o + 32 * b + 1]
+                    z = 4 * C * w + p
+                    ts(wt[:, z:z + 128 * b - 3:4], ps(bv, 32 * b), sc, None, A.is_lt, None, (rv, trn), pl(w, p))
+                    ts(wt[:, z + 128 * b:4 * C * (w + 1):4], T.ps[:, 512 * bv + 32 * b:512 * bv + C], sc, None, A.is_le, None, (rv, trn), pl(w, p))
+                    if par and b % 2: word(w)
+                if ty and not par:
+                    scan(T.dd[:], ps(5), T.k16[:], ("ps5", "k16"), "dd")
+                    ts(T.aw[:], dv, B16 + 48, None, A.add, None, "dd", "aw")
+            word(3)
+            word(4)
+        if t == 0:
+            early_spread(range(2, 8))
+            for k in range(4):
+                ts(T.kt[:, k * KW + k:(k + 1) * KW:4], T.ij[:, 0:128], col(0), None, A.is_equal, None, ("ij", "f0"), "kt%d" % k)
+            last_constants()
+        ts(T.bs[:], ps(1), 0.0625, -6.0, A.mult, A.add, "ps1", "bs")
+        op("v", lambda: V.tensor_copy(T.cs[:].indirect(T.aw[:]), T.bs[:]), ("bs", "aw"), "cs")
+        ts(T.cd[:, 0:4 * C:4], T.cs[:], MAGIC, MAGIC, A.add, A.subtract, "cs", "cd0")
+        tt(T.cd[:, 1:4 * C:4], T.cs[:], T.cd[:, 0:4 * C:4], A.subtract, ("cs", "cd0"), "cd1")
+        qz(T.qc[:], T.qcs[:], T.cd[:], ("cd0", "cd1", "cdz"), "qc")
+        bb = (0, 2, 3, 4, 6, 7, 0, 2)
+
+        def table(k):
+            mm(bb[k], C, *kk(9 + k), T.qc[:], T.qcs[:], ("qc", "kc%d" % (9 + k)))
+
+        def keep(k):
+            act(T.cw[:, C * k:C * k + C], ps(bb[k]), F.Copy, "ps%d" % bb[k], "cw%d" % k)
+
+        for k in range(2 if t == 0 else 6):
+            table(k)
+        keep(0)
+        keep(1)
+        keys = ((T.key0, "key0"), (T.key1, "key1"))
+
+        def grow(k):
+            (a, an), (b, bn) = keys[k % 2], keys[1 - k % 2]
+            op("v", lambda: V.tensor_tensor(b[:], T.cw[:, C * k:C * k + C].indirect(T.nl[:]), a[:], A.add), ("cw%d" % k, "nl", an), bn)
+
+        grow(0)
+        fb = (3, 4, 6, 7)
+        for k in range(1, 8):
+            kr, kn = keys[k % 2]
+            scan(T.col[:], kr[:], T.k96[:], (kn, "k96"), "col")
+            ts(T.cb[:, 0:1], T.col[:, 287:288], B96 - 0.5, None, A.add, None, "col", "cb")
+            act(ct[:, 2:4 * C:4], kr[:], F.Sign, (kn, "cb"), "ct2", bias=T.cb[:, 0:1], scale=-1.0)
+            for p in range(2):
+                ts(ct[:, p:4 * C:4], kr[:], -B96, T.col[:, 96 * p + 95:96 * p + 96], A.add, A.is_lt, (kn, "col"), "ct%d" % p)
+            for h in range(2):
+                a, b = H * h, H * h + H
+                qz(T.qt[:, a:b], T.qts[:, a:b], ct[:, 4 * a:4 * b], ("ct0", "ct1", "ct2", "ctz"), "qt%d" % h)
+                mm((5, 1)[h], H, *kk(8), T.qt[:, a:b], T.qts[:, a:b], ("qt%d" % h, "kc8"))
+            scan(T.dd[:, 0:H], ps(5, H), T.k16[:, 0:H], ("ps5", "k16"), "dd")
+            if k > 1:
+                tt(T.na[:], T.na[:], T.nf[:], A.add, ("na", "nf"), "na")
+            if t == 0:
+                for i in {1: (11, 12), 2: (13, 14, 0), 3: (15, 16, 1), 4: (2, 3)}.get(k, ()):
+                    kz(i)
+            if k <= 3:
+                if t == 0:
+                    table(2 * k)
+                    table(2 * k + 1)
+                elif k == 1:
+                    table(6)
+                    table(7)
+                keep(2 * k)
+                keep(2 * k + 1)
+            if k == 2:
+                op("v", lambda: V.tensor_copy(T.of[:].indirect(T.aw[:]), T.ij[:]), ("ij", "aw"), "of")
+            if k == 3:
+                scan(T.kr[:], T.of[:], T.k16[:], ("of", "k16"), "kr")
+                ts(T.ow[:], T.kr[:, 15:C:16], B16, None, A.add, None, "kr", "ow")
+            if k in (4, 5):
+                for b in (2 * k - 8, 2 * k - 7):
+                    mm(fb[b], C, *kk(b), lc[:], ls[:], ln + ("kc%d" % b,))
+                    act(T.ff[:, C * b:C * b + C], ps(fb[b]), F.Copy, "ps%d" % fb[b], "ff%d" % b)
+            if k in (6, 7):
+                for b in (2 * k - 12, 2 * k - 11):
+                    op("s", lambda: S.activation(T.fs[:, C * b:C * b + C], T.ff[:, C * b:C * b + C].indirect(T.ow[:]), F.Copy), ("ff%d" % b, "ow"), "fs%d" % b)
+            scan(T.dd[:, H:C], ps(1, H), T.k16[:, H:C], ("ps1", "k16"), "dd")
+            if k < 7 or t:
+                ts(T.nl[:], dv, B16 + 48, None, A.add, None, "dd", "nl")
+            if k < 7:
+                grow(k)
+            ts(T.nf[:], dv, B16 + 48, T.gm[:, k:k + 1], A.add, A.mult, ("dd", "gm"), "nf")
+        tt(T.na[:], T.na[:], T.nf[:], A.add, ("na", "nf"), "na")
+        cp(T.nz[:], T.na[:], "na", "nz")
+        zc, zs = T["zc%d" % t], T["zs%d" % t]
+        for b in (0, 1):
+            cp(T.zt[:, b:4 * C:4], T.fs[:, C * b:C * b + C].indirect(T.nz[:]), ("fs%d" % b, "nz"), "zt%d" % b)
+        for b in (2, 3):
+            op("s", lambda: S.activation(T.zt[:, b:4 * C:4], T.fs[:, C * b:C * b + C].indirect(T.nz[:]), F.Copy), ("fs%d" % b, "nz"), "zt%d" % b)
+        qz(zc[:], zs[:], T.zt[:], ["zt%d" % b for b in range(4)], "zc")
+        for b in range(4):
+            for h in range(2):
+                w = 128 * (b + 4 * h)
+                mm(2 * b + h, C, T.wk[:, w:w + 128], T.wp[:, w:w + 128], zc[:], zs[:], ("zc", "wk", "wp"))
+        op("v", lambda: V.tensor_copy(T.nv[:].indirect(T.nz[:]), T.ij[:]), ("ij", "nz"), "nv")
+        cp(T.kr[:], T.nv[:].indirect(T.aw[:]), ("nv", "aw"), "kr")
+        if t:
+            grow(7)
+        scan(T.dd[:], T.kr[:], T.k16[:], ("kr", "k16"), "dd")
+        ts(T.kw[:], dv, B16, None, A.add, None, "dd", "kw")
+        for b in range(4):
+            act(T.y1[:, C * b:C * b + C], ps(2 * b), F.Copy, "ps%d" % (2 * b), "y1%d" % b)
+            tt(T.ym[:, C * b:C * b + C], ps(2 * b + 1), T.y1[:, C * b:C * b + C], A.max, ("ps%d" % (2 * b + 1), "y1%d" % b), "ym%d" % b)
+        for b in (0, 2, 3, 1):
+            o, i = T.yt[:, b:4 * C:4], T.ym[:, C * b:C * b + C].indirect(T.kw[:])
+            rd, wr = ("ym%d" % b, "kw"), "yt%d" % b
+            if b % 2: op("v", lambda: V.tensor_scalar(o, i, 0.03125, None, A.mult), rd, wr)
+            else: op("s", lambda: S.activation(o, i, F.Copy, scale=0.03125), rd, wr)
+        qn = ("qc%d" % t, "qs%d" % t)
+        qz(T[qn[0]][:], T[qn[1]][:], T.yt[:], ["yt%d" % b for b in range(4)], qn)
+        send(qn, ("bc%d" % t, "bs%d" % t), "ay%d" % t, peer)
+        for b in range(4):
+            mm(b, C, *kk(b), xc[:], xs[:], xn + ("kc%d" % b,), True, False)
+        if t == 1:
+            tt(T.to[0:1, :], T.key0[0:1, :], T.ij[0:1, :], A.add, ("key0", "ij"), "to")
+            ts(T.to[0:1, :], T.to[0:1, :], 1.0 / 512, 1152.0, A.mult, A.add, "to", "to")
+            ld("y", T.tot[:], T.to[0:1, :], "tot", "to")
+            qz(T.vq[:], T.vs[:], T.vt[:], "vt", "vq")
+        xt = T["xt%d" % (t + 1)]
+        for b in range(4):
+            mm(b, C, *kk(b), T["bc%d" % t][:], T["bs%d" % t][:], ("bc%d" % t, "bs%d" % t, "kc%d" % b), False, True)
+        for b in range(4):
+            if b % 2: act(xt[:, b:4 * C:4], ps(b), F.Copy, "ps%d" % b, "x%d" % b)
+            else: cp(xt[:, b:4 * C:4], ps(b), "ps%d" % b, "x%d" % b)
+        nx = ("xc%d" % (t + 1), "xs%d" % (t + 1))
+        qz(T[nx[0]][:], T[nx[1]][:], xt[:], ["x%d" % b for b in range(4)], nx)
+        if t == 0:
+            send(nx, ("lc1", "ls1"), "ax1", peers[1])
+    ld("y", T.oc[:], T.xc2[:].bitcast(dt.uint8), "oc", "xc2")
+    for k in range(4):
+        ld("s" if k % 2 else "y", T.osc[4 * k:4 * k + 4, :], T.xs2[32 * k:32 * k + 4, :], "osc%d" % k, "xs2")
+    mm(4, C, T.vq[:], T.vs[:], T.xc2[:], T.xs2[:], ("xc2", "xs2", "vq"))
+    act(T.yo[:], ps(4), F.Copy, "ps4", "yo")
+    ld("s", T.y[:], T.yo[:], "yout", "yo")
+    for q in "vstg":
+        g.wait_ge(T.sem["c" + q], cnt[q])
+    for i in range(ndma[0]):
+        g.wait_ge(T.sem[DMAS[i]], 16)
+    g.wait_ge(T.sem.sent, sent[0])
+    for t in range(2):
+        for s in ("ax", "ay"):
+            g.wait_ge(T.sem[s + "%d" % t], 2 * len(topo.engines(core, peers[t])))

@@ -1,7 +1,7 @@
 from concourse.mybir import dt, AluOpType as A, ActivationFunctionType as F
 
 C = 288
-H = C // 2
+H = 160
 KW = 512
 B16, B96 = 2.0 ** 18, 2.0 ** 21
 BIG, TINY, MAGIC = 1e29, 2.0 ** -119, 1.5 * 2.0 ** 23
@@ -27,16 +27,16 @@ for _t in range(2):
 for _n, _c, _d in (("wk", 1024, MXC), ("wp", 1024, PL), ("ut", 512, "bfloat16"), ("vt", 512, "bfloat16"), ("uq", 128, MXC), ("us", 128, PL),
                    ("vq", 128, MXC), ("vs", 128, PL), ("up", 640, MXC), ("ups", 640, PL), ("kt", NK * 512, "bfloat16"), ("kc", NK * 128, MXC),
                    ("ks", NK * 128, PL), ("tm2", 512, "bfloat16"), ("ui", 40, "int32"), ("ul", 40, "uint16"), ("pi", 2, "int32"), ("pj", 4, "int32"),
-                   ("fc", 16, "float32"), ("gm", 8, "float32"), ("bcm", 8, "float32"), ("ij", C, "float32"), ("rowx", C, "float32"),
+                   ("fc", 20, "float32"), ("mk", 4, "float32"), ("bcm", 8, "float32"), ("ij", C, "float32"), ("rowx", C, "float32"),
                    ("row16", C, "float32"), ("row32", C, "float32"), ("row96", C, "float32"), ("rowog", 128, "float32"), ("hown", C, "float32"),
                    ("hb", C, "float32"), ("k16", C, "float32"), ("k96", C, "float32"), ("t1", C, "float32"), ("t2", C, "float32"),
                    ("t3", C, "float32"), ("t4", C, "float32"), ("wo", 4 * C, "bfloat16"), ("qo", C, MXC), ("qos", C, PL), ("om", C, "float32"),
                    ("wa", 20 * C, "bfloat16"), ("wb", 20 * C, "bfloat16"), ("qa", 5 * C, MXC), ("qas", 5 * C, PL), ("qb", 5 * C, MXC),
-                   ("qbs", 5 * C, PL), ("rm", 4 * C, "float32"), ("tr", 4 * C, "float32"), ("ds", 6 * C, "float32"), ("dd", C, "float32"),
-                   ("key0", C, "float32"), ("key1", C, "float32"), ("col", C, "float32"), ("cb", 2, "float32"), ("nl", 18, "uint16"),
-                   ("nf", 18, "float32"), ("na", 18, "float32"), ("nz", 18, "uint16"), ("aw", 18, "uint16"), ("ow", 18, "uint16"),
-                   ("kw", 18, "uint16"), ("bs", C, "float32"), ("cs", C, "float32"), ("of", C, "float32"), ("nv", C, "float32"),
-                   ("kr", C, "float32"), ("cd", 4 * C, "bfloat16"), ("qc", C, MXC), ("qcs", C, PL), ("cw", 8 * C, "float32"),
+                   ("qbs", 5 * C, PL), ("rm", 4 * C, "float32"), ("tr", 4 * C, "float32"), ("ds", 8 * C, "float32"), ("dd", C, "float32"),
+                   ("de", C, "float32"), ("key0", C, "float32"), ("key1", C, "float32"), ("col", C, "float32"), ("nl", 18, "uint16"),
+                   ("nf", 18, "float32"), ("ne", 18, "float32"), ("no", 18, "float32"), ("nz", 18, "uint16"), ("aw", 18, "uint16"),
+                   ("ow", 18, "uint16"), ("kw", 18, "uint16"), ("bs", C, "float32"), ("cs", C, "float32"), ("of", C, "float32"),
+                   ("nv", C, "float32"), ("kr", C, "float32"), ("cd", 4 * C, "bfloat16"), ("qc", C, MXC), ("qcs", C, PL), ("cw", 8 * C, "float32"),
                    ("ct", 4 * C, "bfloat16"), ("qt", C, MXC), ("qts", C, PL), ("ff", 4 * C, "bfloat16"), ("fs", 4 * C, "bfloat16"),
                    ("zt", 4 * C, "bfloat16"), ("y1", 4 * C, "float32"), ("ym", 4 * C, "bfloat16"), ("yt", 4 * C, "bfloat16"),
                    ("yo", C, "float32"), ("to", C, "float32")):
@@ -168,10 +168,10 @@ def rank_program(g, core, T, topo):
     def picker(row, rn, c0, c1, step):
         for t, n, c in ((T.t1, "t1", c0), (T.t2, "t2", c1)):
             act(t[:], row, F.Abs, (rn, "f%d" % c), n, bias=col(c))
-            act(t[:], t[:], F.Relu, n, n, bias=T.fc[:, 14:15] if step == B16 else T.fc[:, 15:16], scale=-step)
+            act(t[:], t[:], F.Relu, n, n, bias=col(14 if step == B16 else 15), scale=-step)
 
-    ms(T.fc[:, 14:15], B16, "f14")
-    ms(T.fc[:, 15:16], B96, "f15")
+    for i, x in ((13, TINY), (16, -TINY), (14, B16), (15, B96)):
+        ms(col(i), x, "f%d" % i)
     ms(T.ui[:, 32:40], 0, "uz")
     cp(col(0), T.pi[:, 0:1], "pi", "f0")
     for i, (o, k) in enumerate(((A.bitwise_and, 15), (A.bitwise_and, 31), (A.arith_shift_right, 4), (A.arith_shift_right, 5))):
@@ -185,8 +185,7 @@ def rank_program(g, core, T, topo):
     for w, (lo, hi, val) in ((0, (0, 128, 512.0)), (1, (0, 128, 512.0)), (3, (0, 128, -512.0)), (2, (0, 128, 0.0)), (2, (96, 128, 512.0))):
         ms(T.kt[lo:hi, 7 * KW + w:8 * KW:4], val, "kt7")
     cp(T.ul[:], T.ui[:], ("ui", "uz"), "ul")
-    for k in (8, 0, 1, 2, 3):
-        ms(T.kt[:, k * KW:(k + 1) * KW], 0.0, "kt%d" % k)
+    ms(T.kt[:, 8 * KW:9 * KW], 0.0, "kt8")
     qz(T.uq[:], T.us[:], T.ut[:], "ut", ("uq", "us"))
 
     def upick(i):
@@ -200,6 +199,13 @@ def rank_program(g, core, T, topo):
     send(("xc0", "xs0"), ("lc0", "ls0"), "ax0", peers[0])
     iota(T.row32[:], [[0, 9], [1, 32]], 0, 0, "row32")
     iota(T.row96[:], [[0, 3], [1, 96]], 0, 0, "row96")
+    for t in range(4):
+        iota(T.tm2[:, t:512:4], [[0, 128]], 8192 if t < 2 else 0, 0, "tm2")
+    for t in range(2, 4):
+        iota(T.cd[:, t:4 * C:4], [[0, C]], 0, 0, "cdz")
+    iota(T.ct[:, 3:4 * C:4], [[0, C]], 0, 0, "ctz")
+    for k in range(4):
+        iota(T.kt[:, k * KW:(k + 1) * KW], [[0, KW]], 0, 0, "kt%d" % k)
     kz(7)
     tt(T.k16[:], T.t1[:], T.t2[:], A.subtract, ("t1", "t2"), "k16")
     ts(T.k16[:, 15:C:16], T.k16[:, 15:C:16], -2.0 * B16, None, A.add, None, "k16", "k16")
@@ -207,28 +213,25 @@ def rank_program(g, core, T, topo):
     ts(T.t4[:, 0:128], T.rowog[:], col(12), None, A.is_equal, None, ("rowog", "f12"), "t4")
     for i in range(4):
         upick(i)
-    for k, w in ((4, (1.0, 1.0)), (5, (0.5, 0.5)), (6, (0.5, -1.0))):
+    for k, w in ((4, (1.0, 1.0)), (5, (0.5, 0.5)), (6, (1.0, -1.0))):
         for t in range(4):
             src, n = (T.t3, "t3") if t < 2 else (T.t4, "t4")
             act(T.kt[:, k * KW + t:(k + 1) * KW:4], src[:, 0:128], F.Copy, n, "kt%d" % k, scale=w[t % 2])
     act(T.hb[:], T.row32[:], F.Identity, ("row32", "f7"), "hb", bias=col(7), scale=-BIG)
 
-    def early_spread(ks):
+    def spread(ks):
         for k in ks:
             act(T.kt[:, (9 + k) * KW:(10 + k) * KW], T.tm2[:], F.Copy, ("tm2", "bcm"), "kt%d" % (9 + k), scale=T.bcm[:, k:k + 1])
 
     def late_constants():
-        ts(T.gm[:], T.ij[:, 0:8], col(3), None, A.is_equal, None, ("ij", "f1"), "gm")
+        for m in range(2):
+            ts(T.mk[:, m:m + 1], col(2), 15.5, None, (A.is_lt, A.is_gt)[m], None, "f1", "mk")
+            ts(T.mk[:, m + 2:m + 3], col(2), 15.5, B16 + 48, (A.is_lt, A.is_gt)[m], A.mult, "f1", "mk")
         ts(T.bcm[:], T.ij[:, 0:8], 16.0, col(0), A.mult, A.is_equal, ("ij", "f0"), "bcm")
-        for t in range(4):
-            ms(T.tm2[:, t:512:4], 8192.0 if t < 2 else 0.0, "tm2")
         for t, w in enumerate((1.0, 1.0, 0.5)):
             ms(T.kt[0:96, 8 * KW + t:9 * KW:4], w, "kt8")
-        for t in range(2, 4):
-            ms(T.cd[:, t:4 * C:4], 0.0, "cdz")
-        ms(T.ct[:, 3:4 * C:4], 0.0, "ctz")
         picker(T.row96[:], "row96", 8, 9, B96)
-        early_spread((0, 1))
+        spread((0, 1))
         for k in (4, 5, 6):
             kz(k)
 
@@ -236,12 +239,13 @@ def rank_program(g, core, T, topo):
         for i in (9, 10, 8):
             kz(i)
         tt(T.k96[:], T.t1[:], T.t2[:], A.subtract, ("t1", "t2"), "k96")
-        ts(T.k96[:, 95:C:96], T.k96[:, 95:C:96], -2.0 * B96, None, A.add, None, "k96", "k96")
+        ts(T.k96[:, 95:192:96], T.k96[:, 95:192:96], -2.0 * B96, None, A.add, None, "k96", "k96")
+        ts(T.k96[:, 287:C], T.k96[:, 287:C], -B96 - 0.5, None, A.add, None, "k96", "k96")
 
-    dv = T.dd[:, 15:C:16]
     wo, ct = T.wo, T.ct
     for t in range(2):
         peer = peers[t]
+        dv = T.dd[:, 15:C:16]
         xc, xs = T["xc%d" % t], T["xs%d" % t]
         xn = ("xc%d" % t, "xs%d" % t)
         lc, ls = T["lc%d" % t], T["ls%d" % t]
@@ -266,55 +270,79 @@ def rank_program(g, core, T, topo):
         tt(T.key0[:], ps(4), T.ij[:], A.subtract, ("ps4", "ij"), "key0")
         ts(T.nl[:], dv, -1.0 / 512, 287.0 - B16 / 512, A.mult, A.add, "dd", "nl")
         ts(T.nf[:], dv, -1.0 / 512, 287.0 - B16 / 512, A.mult, A.add, "dd", "nf")
-        ts(T.na[:], T.nf[:], T.gm[:, 0:1], None, A.mult, None, ("nf", "gm"), "na")
+        ts(T.ne[0:32, :], T.nf[0:32, :], T.mk[0:32, 0:1], None, A.mult, None, ("nf", "mk"), "ne")
         banks = ((5, 7), (6, 0), (1, 3), (2, 4))
         for k in range(4):
             for b in banks[k]:
                 mm(b, C, T.up[:, 128 * k:128 * k + 128], T.ups[:, 128 * k:128 * k + 128], lc[:], ls[:], ln + ("up%d" % k, "ups%d" % k))
-        for ty in range(2):
-            wt, qn, pb = (T.wa, "qa", 5) if ty == 0 else (T.wb, "qb", 1)
-            qc, qs = T[qn], T[qn + "s"]
 
-            def pl(w, p):
-                return "w%s%d.%d" % (qn, w, p)
+        def side(ty):
+            return (T.wa, "qa", 5) if ty == 0 else (T.wb, "qb", 1)
 
-            def word(w):
-                c = (4, 4, 4, 5, 6)[w]
-                qz(qc[:, C * w:C * w + C], qs[:, C * w:C * w + C], wt[:, 4 * C * w:4 * C * w + 4 * C], [pl(w, p) for p in range(4)], qn + "%d" % w)
-                mm(pb, C, *kk(c), qc[:, C * w:C * w + C], qs[:, C * w:C * w + C], (qn + "%d" % w, "kc%d" % c), w == 0, w == 4)
+        def pl(ty, w, p):
+            return "w%d.%d.%d" % (ty, w, p)
 
+        def rows(ty):
+            wt = side(ty)[0]
             for par in range(2):
                 k = 2 * ty + par
-                bv, bw = banks[k]
-                rv, trn, o = "ps%d" % bv, "tr%d" % k, C * k
-                tt(T.rm[:, o:o + C], ps(bv), T.hb[:], A.max, (rv, "hb"), "rm%d" % k)
-                op("v", lambda: V.transpose(T.tr[:, o:o + C], T.rm[:, o:o + C]), "rm%d" % k, trn)
-                for i, (b, w, p) in enumerate(((0, 3, 0), (1, 3, 1), (8, 4, 0))):
-                    d0 = C * (3 * par + i)
-                    dn = "ds%d" % (3 * par + i)
-                    act(T.ds[:, d0:d0 + C], ps(bw), F.Identity, ("ps%d" % bw, trn), dn, bias=T.tr[:, o + 32 * b:o + 32 * b + 1], scale=-1.0)
-                    z = 4 * C * w + 2 * par + p
-                    if b: act(wt[:, z:z + 128 * b - 3:4], T.ds[:, d0:d0 + 32 * b], F.Sign, (dn, "tny"), pl(w, 2 * par + p), bias=-TINY)
-                    act(wt[:, z + 128 * b:4 * C * (w + 1):4], T.ds[:, d0 + 32 * b:d0 + C], F.Sign, (dn, "tny"), pl(w, 2 * par + p), bias=TINY)
-                tt(wt[:, 16 * C + 2 * par + 1:20 * C:4], ps(bv), T.tr[:, o:o + C], A.is_equal, (rv, trn), pl(4, 2 * par + 1))
-                for b in range(2, 8):
-                    w, p = (b - 2) // 2, 2 * par + b % 2
-                    sc = T.tr[:, o + 32 * b:o + 32 * b + 1]
-                    z = 4 * C * w + p
-                    ts(wt[:, z:z + 128 * b - 3:4], ps(bv, 32 * b), sc, None, A.is_lt, None, (rv, trn), pl(w, p))
-                    ts(wt[:, z + 128 * b:4 * C * (w + 1):4], T.ps[:, 512 * bv + 32 * b:512 * bv + C], sc, None, A.is_le, None, (rv, trn), pl(w, p))
-                    if par and b % 2: word(w)
-                if ty and not par:
-                    scan(T.dd[:], ps(5), T.k16[:], ("ps5", "k16"), "dd")
-                    ts(T.aw[:], dv, B16 + 48, None, A.add, None, "dd", "aw")
-            word(3)
-            word(4)
+                o = C * k
+                tt(T.rm[:, o:o + C], ps(banks[k][0]), T.hb[:], A.max, ("ps%d" % banks[k][0], "hb"), "rm%d" % k)
+                op("v", lambda: V.transpose(T.tr[:, o:o + C], T.rm[:, o:o + C]), "rm%d" % k, "tr%d" % k)
+            for w in range(2):
+                for par in range(2):
+                    k = 2 * ty + par
+                    bw = banks[k][1]
+                    for i in range(2):
+                        b, z = (0, 1, 7, 8)[2 * w + i], 4 * C * w + 2 * par + i
+                        act(T.ds[:, z:4 * C * (w + 1):4], ps(bw), F.Identity, ("ps%d" % bw, "tr%d" % k), "ds%d.%d" % (w, 2 * par + i),
+                            bias=T.tr[:, C * k + 32 * b:C * k + 32 * b + 1], scale=-1.0)
+                for st, lo, hi, s in (((1, 32, C, 1), (2, 0, 32, 1), (-2, 0, 32, -1)),
+                                      ((1, 0, 224, -1), (2, 224, 256, 1), (-2, 224, 256, -1), (1, 256, C, 1)))[w]:
+                    f = 4 * C * w + (st < 0)
+                    act(wt[:, 12 * C + f + 4 * lo:12 * C + 4 * C * w + 4 * hi:abs(st)], T.ds[:, f + 4 * lo:4 * C * w + 4 * hi:abs(st)], F.Sign,
+                        ["ds%d.%d" % (w, p) for p in range(4)] + ["f13", "f16"], [pl(ty, 3 + w, p) for p in range(4)], bias=col(13 if s > 0 else 16))
+
+        def word(ty, w):
+            wt, qn, pb = side(ty)
+            qc, qs = T[qn], T[qn + "s"]
+            c = (4, 4, 6, 5, 5)[w]
+            qz(qc[:, C * w:C * w + C], qs[:, C * w:C * w + C], wt[:, 4 * C * w:4 * C * w + 4 * C], [pl(ty, w, p) for p in range(4)], qn + "%d" % w)
+            mm(pb, C, *kk(c), qc[:, C * w:C * w + C], qs[:, C * w:C * w + C], (qn + "%d" % w, "kc%d" % c), w == 0, w == 4)
+
+        def blocks(ty, par):
+            wt = side(ty)[0]
+            k = 2 * ty + par
+            bv = banks[k][0]
+            rd, o = ("ps%d" % bv, "tr%d" % k), C * k
+            tt(wt[:, 8 * C + 2 * par + 1:12 * C:4], ps(bv), T.tr[:, o:o + C], A.is_equal, rd, pl(ty, 2, 2 * par + 1))
+            for b in range(2, 7):
+                w, p = (b - 2) // 2, 2 * par + b % 2
+                sc = T.tr[:, o + 32 * b:o + 32 * b + 1]
+                z = 4 * C * w + p
+                ts(wt[:, z:z + 128 * b - 3:4], ps(bv, 32 * b), sc, None, A.is_lt, None, rd, pl(ty, w, p))
+                ts(wt[:, z + 128 * b:4 * C * (w + 1):4], T.ps[:, 512 * bv + 32 * b:512 * bv + C], sc, None, A.is_le, None, rd, pl(ty, w, p))
+                if par and (b % 2 or b == 6): word(ty, w)
+
+        rows(0)
+        blocks(0, 0)
+        rows(1)
+        blocks(0, 1)
+        blocks(1, 0)
+        word(0, 3)
+        word(0, 4)
+        blocks(1, 1)
+        scan(T.dd[:], ps(5), T.k16[:], ("ps5", "k16"), "dd")
+        ts(T.aw[:], dv, B16 + 64, None, A.add, None, "dd", "aw")
+        word(1, 3)
+        word(1, 4)
+        op("v", lambda: V.tensor_copy(T.of[:].indirect(T.aw[:]), T.ij[:]), ("ij", "aw"), "of")
         if t == 0:
-            early_spread(range(2, 8))
+            spread(range(2, 8))
             for k in range(4):
                 ts(T.kt[:, k * KW + k:(k + 1) * KW:4], T.ij[:, 0:128], col(0), None, A.is_equal, None, ("ij", "f0"), "kt%d" % k)
             last_constants()
-        ts(T.bs[:], ps(1), 0.0625, -6.0, A.mult, A.add, "ps1", "bs")
+        ts(T.bs[:], ps(1), 0.0625, -5.0, A.mult, A.add, "ps1", "bs")
         op("v", lambda: V.tensor_copy(T.cs[:].indirect(T.aw[:]), T.bs[:]), ("bs", "aw"), "cs")
         ts(T.cd[:, 0:4 * C:4], T.cs[:], MAGIC, MAGIC, A.add, A.subtract, "cs", "cd0")
         tt(T.cd[:, 1:4 * C:4], T.cs[:], T.cd[:, 0:4 * C:4], A.subtract, ("cs", "cd0"), "cd1")
@@ -325,10 +353,13 @@ def rank_program(g, core, T, topo):
             mm(bb[k], C, *kk(9 + k), T.qc[:], T.qcs[:], ("qc", "kc%d" % (9 + k)))
 
         def keep(k):
-            act(T.cw[:, C * k:C * k + C], ps(bb[k]), F.Copy, "ps%d" % bb[k], "cw%d" % k)
+            if k: act(T.cw[:, C * k:C * k + C], ps(bb[k]), F.Copy, "ps%d" % bb[k], "cw%d" % k)
+            else: cp(T.cw[:, 0:C], ps(bb[0]), "ps%d" % bb[0], "cw0")
 
         for k in range(2 if t == 0 else 6):
             table(k)
+        scan(T.kr[:], T.of[:], T.k16[:], ("of", "k16"), "kr")
+        ts(T.ow[:], T.kr[:, 15:C:16], B16, None, A.add, None, "kr", "ow")
         keep(0)
         keep(1)
         keys = ((T.key0, "key0"), (T.key1, "key1"))
@@ -342,17 +373,16 @@ def rank_program(g, core, T, topo):
         for k in range(1, 8):
             kr, kn = keys[k % 2]
             scan(T.col[:], kr[:], T.k96[:], (kn, "k96"), "col")
-            ts(T.cb[:, 0:1], T.col[:, 287:288], B96 - 0.5, None, A.add, None, "col", "cb")
-            act(ct[:, 2:4 * C:4], kr[:], F.Sign, (kn, "cb"), "ct2", bias=T.cb[:, 0:1], scale=-1.0)
+            act(ct[:, 2:4 * C:4], kr[:], F.Sign, (kn, "col"), "ct2", bias=T.col[:, 287:288], scale=-1.0)
             for p in range(2):
                 ts(ct[:, p:4 * C:4], kr[:], -B96, T.col[:, 96 * p + 95:96 * p + 96], A.add, A.is_lt, (kn, "col"), "ct%d" % p)
             for h in range(2):
-                a, b = H * h, H * h + H
+                a, b = (0, H, C)[h:h + 2]
                 qz(T.qt[:, a:b], T.qts[:, a:b], ct[:, 4 * a:4 * b], ("ct0", "ct1", "ct2", "ctz"), "qt%d" % h)
-                mm((5, 1)[h], H, *kk(8), T.qt[:, a:b], T.qts[:, a:b], ("qt%d" % h, "kc8"))
-            scan(T.dd[:, 0:H], ps(5, H), T.k16[:, 0:H], ("ps5", "k16"), "dd")
-            if k > 1:
-                tt(T.na[:], T.na[:], T.nf[:], A.add, ("na", "nf"), "na")
+                mm((5, 1)[h], b - a, *kk(8), T.qt[:, a:b], T.qts[:, a:b], ("qt%d" % h, "kc8"))
+            dx, dn = ((T.dd, "dd"), (T.de, "de"))[k % 2]
+            dv = dx[:, 15:C:16]
+            scan(dx[:, 0:H], ps(5, H), T.k16[:, 0:H], ("ps5", "k16"), dn)
             if t == 0:
                 for i in {1: (11, 12), 2: (13, 14, 0), 3: (15, 16, 1), 4: (2, 3)}.get(k, ()):
                     kz(i)
@@ -365,11 +395,6 @@ def rank_program(g, core, T, topo):
                     table(7)
                 keep(2 * k)
                 keep(2 * k + 1)
-            if k == 2:
-                op("v", lambda: V.tensor_copy(T.of[:].indirect(T.aw[:]), T.ij[:]), ("ij", "aw"), "of")
-            if k == 3:
-                scan(T.kr[:], T.of[:], T.k16[:], ("of", "k16"), "kr")
-                ts(T.ow[:], T.kr[:, 15:C:16], B16, None, A.add, None, "kr", "ow")
             if k in (4, 5):
                 for b in (2 * k - 8, 2 * k - 7):
                     mm(fb[b], C, *kk(b), lc[:], ls[:], ln + ("kc%d" % b,))
@@ -377,14 +402,19 @@ def rank_program(g, core, T, topo):
             if k in (6, 7):
                 for b in (2 * k - 12, 2 * k - 11):
                     op("s", lambda: S.activation(T.fs[:, C * b:C * b + C], T.ff[:, C * b:C * b + C].indirect(T.ow[:]), F.Copy), ("ff%d" % b, "ow"), "fs%d" % b)
-            scan(T.dd[:, H:C], ps(1, H), T.k16[:, H:C], ("ps1", "k16"), "dd")
+            scan(dx[:, H:C], ps(1, C - H), T.k16[:, H:C], ("ps1", "k16"), dn)
             if k < 7 or t:
-                ts(T.nl[:], dv, B16 + 48, None, A.add, None, "dd", "nl")
+                ts(T.nl[:], dv, B16 + 48, None, A.add, None, dn, "nl")
             if k < 7:
                 grow(k)
-            ts(T.nf[:], dv, B16 + 48, T.gm[:, k:k + 1], A.add, A.mult, ("dd", "gm"), "nf")
-        tt(T.na[:], T.na[:], T.nf[:], A.add, ("na", "nf"), "na")
-        cp(T.nz[:], T.na[:], "na", "nz")
+            p0, m = 32 * (k // 2), k % 2
+            p1 = p0 + 32
+            nb, nn = ((T.ne, "ne"), (T.no, "no"))[m]
+            if k < 7: act(nb[p0:p1, :], dv[p0:p1, :], F.Identity, (dn, "mk"), nn, bias=T.mk[p0:p1, 2 + m:3 + m], scale=T.mk[p0:p1, m:m + 1])
+            else: ts(nb[p0:p1, :], dv[p0:p1, :], B16 + 48, T.mk[p0:p1, 1:2], A.add, A.mult, (dn, "mk"), nn)
+        tt(T.nf[:], T.ne[:], T.no[:], A.add, ("ne", "no"), "nf")
+        cp(T.nz[:], T.nf[:], "nf", "nz")
+        dv = T.dd[:, 15:C:16]
         zc, zs = T["zc%d" % t], T["zs%d" % t]
         for b in (0, 1):
             cp(T.zt[:, b:4 * C:4], T.fs[:, C * b:C * b + C].indirect(T.nz[:]), ("fs%d" % b, "nz"), "zt%d" % b)
@@ -401,14 +431,24 @@ def rank_program(g, core, T, topo):
             grow(7)
         scan(T.dd[:], T.kr[:], T.k16[:], ("kr", "k16"), "dd")
         ts(T.kw[:], dv, B16, None, A.add, None, "dd", "kw")
-        for b in range(4):
+
+        def largest(b):
             act(T.y1[:, C * b:C * b + C], ps(2 * b), F.Copy, "ps%d" % (2 * b), "y1%d" % b)
             tt(T.ym[:, C * b:C * b + C], ps(2 * b + 1), T.y1[:, C * b:C * b + C], A.max, ("ps%d" % (2 * b + 1), "y1%d" % b), "ym%d" % b)
-        for b in (0, 2, 3, 1):
+
+        def put(b, v):
             o, i = T.yt[:, b:4 * C:4], T.ym[:, C * b:C * b + C].indirect(T.kw[:])
             rd, wr = ("ym%d" % b, "kw"), "yt%d" % b
-            if b % 2: op("v", lambda: V.tensor_scalar(o, i, 0.03125, None, A.mult), rd, wr)
+            if v: op("v", lambda: V.tensor_scalar(o, i, 0.03125, None, A.mult), rd, wr)
             else: op("s", lambda: S.activation(o, i, F.Copy, scale=0.03125), rd, wr)
+
+        for b in range(3):
+            largest(b)
+        put(0, True)
+        largest(3)
+        put(1, False)
+        put(2, False)
+        put(3, True)
         qn = ("qc%d" % t, "qs%d" % t)
         qz(T[qn[0]][:], T[qn[1]][:], T.yt[:], ["yt%d" % b for b in range(4)], qn)
         send(qn, ("bc%d" % t, "bs%d" % t), "ay%d" % t, peer)
@@ -423,7 +463,7 @@ def rank_program(g, core, T, topo):
         for b in range(4):
             mm(b, C, *kk(b), T["bc%d" % t][:], T["bs%d" % t][:], ("bc%d" % t, "bs%d" % t, "kc%d" % b), False, True)
         for b in range(4):
-            if b % 2: act(xt[:, b:4 * C:4], ps(b), F.Copy, "ps%d" % b, "x%d" % b)
+            if b % 2 == 0: act(xt[:, b:4 * C:4], ps(b), F.Copy, "ps%d" % b, "x%d" % b)
             else: cp(xt[:, b:4 * C:4], ps(b), "ps%d" % b, "x%d" % b)
         nx = ("xc%d" % (t + 1), "xs%d" % (t + 1))
         qz(T[nx[0]][:], T[nx[1]][:], xt[:], ["x%d" % b for b in range(4)], nx)

@@ -2,6 +2,7 @@ from concourse.mybir import dt, AluOpType as A, ActivationFunctionType as F
 
 C = 288
 H = 160
+PARTS = ((0, H), (H, C))
 KW = 512
 B16, B96 = 2.0 ** 18, 2.0 ** 21
 BIG, TINY, MAGIC = 1e29, 2.0 ** -119, 1.5 * 2.0 ** 23
@@ -32,7 +33,7 @@ for _n, _c, _d in (("wk", 1024, MXC), ("wp", 1024, PL), ("ut", 512, "bfloat16"),
                    ("hb", C, "float32"), ("k16", C, "float32"), ("k96", C, "float32"), ("t1", C, "float32"), ("t2", C, "float32"),
                    ("t3", C, "float32"), ("t4", C, "float32"), ("wo", 4 * C, "bfloat16"), ("qo", C, MXC), ("qos", C, PL), ("om", C, "float32"),
                    ("wa", 20 * C, "bfloat16"), ("wb", 20 * C, "bfloat16"), ("qa", 5 * C, MXC), ("qas", 5 * C, PL), ("qb", 5 * C, MXC),
-                   ("qbs", 5 * C, PL), ("rm", 4 * C, "float32"), ("tr", 4 * C, "float32"), ("ds", 8 * C, "float32"), ("dd", C, "float32"),
+                   ("qbs", 5 * C, PL), ("rm", 4 * C, "float32"), ("tr", 4 * C, "float32"), ("ds", 16 * C, "float32"), ("dd", C, "float32"),
                    ("de", C, "float32"), ("key0", C, "float32"), ("key1", C, "float32"), ("col", C, "float32"), ("nl", 18, "uint16"),
                    ("nf", 18, "float32"), ("ne", 18, "float32"), ("no", 18, "float32"), ("nz", 18, "uint16"), ("aw", 18, "uint16"),
                    ("ow", 18, "uint16"), ("kw", 18, "uint16"), ("bs", C, "float32"), ("cs", C, "float32"), ("of", C, "float32"),
@@ -72,8 +73,8 @@ def rank_program(g, core, T, topo):
             if k in last: toks.append(last[k])
             if k[:2] == "ps": toks += [w for w in readers.get(k, {}).values() if w[3] != me]
         for k in wr:
-            if k in last and not (q == "t" and last[k][3] == "t"): toks.append(last[k])
-            toks += [w for w in readers.get(k, {}).values() if w[3] != me or dma]
+            if k in last and last[k][3] != q: toks.append(last[k])
+            toks += list(readers.get(k, {}).values())
         waits(q, toks)
         ins = fn()
         if dma:
@@ -182,10 +183,9 @@ def rank_program(g, core, T, topo):
         ts(col(i), col(j), a, b, A.mult, A.add, ("f0", "f1"), "f%d" % i)
     act(T.hown[:], T.rowx[:], F.Identity, ("rowx", "f10"), "hown", bias=col(10), scale=BIG)
     picker(T.row16[:], "row16", 5, 6, B16)
-    for w, (lo, hi, val) in ((0, (0, 128, 512.0)), (1, (0, 128, 512.0)), (3, (0, 128, -512.0)), (2, (0, 128, 0.0)), (2, (96, 128, 512.0))):
+    for w, (lo, hi, val) in ((0, (0, 128, 512.0)), (1, (0, 128, 512.0)), (3, (0, 128, -512.0)), (2, (0, 96, 0.0)), (2, (96, 128, 512.0))):
         ms(T.kt[lo:hi, 7 * KW + w:8 * KW:4], val, "kt7")
     cp(T.ul[:], T.ui[:], ("ui", "uz"), "ul")
-    ms(T.kt[:, 8 * KW:9 * KW], 0.0, "kt8")
     qz(T.uq[:], T.us[:], T.ut[:], "ut", ("uq", "us"))
 
     def upick(i):
@@ -228,8 +228,9 @@ def rank_program(g, core, T, topo):
             ts(T.mk[:, m:m + 1], col(2), 15.5, None, (A.is_lt, A.is_gt)[m], None, "f1", "mk")
             ts(T.mk[:, m + 2:m + 3], col(2), 15.5, B16 + 48, (A.is_lt, A.is_gt)[m], A.mult, "f1", "mk")
         ts(T.bcm[:], T.ij[:, 0:8], 16.0, col(0), A.mult, A.is_equal, ("ij", "f0"), "bcm")
-        for t, w in enumerate((1.0, 1.0, 0.5)):
+        for t, w in enumerate((1.0, 1.0, 0.5, 0.0)):
             ms(T.kt[0:96, 8 * KW + t:9 * KW:4], w, "kt8")
+        ms(T.kt[96:128, 8 * KW:9 * KW], 0.0, "kt8")
         picker(T.row96[:], "row96", 8, 9, B96)
         spread((0, 1))
         for k in (4, 5, 6):
@@ -242,7 +243,8 @@ def rank_program(g, core, T, topo):
         ts(T.k96[:, 95:192:96], T.k96[:, 95:192:96], -2.0 * B96, None, A.add, None, "k96", "k96")
         ts(T.k96[:, 287:C], T.k96[:, 287:C], -B96 - 0.5, None, A.add, None, "k96", "k96")
 
-    wo, ct = T.wo, T.ct
+    wo, ct, zt = T.wo, T.ct, T.zt
+    D01 = ("dd0", "dd1")
     for t in range(2):
         peer = peers[t]
         dv = T.dd[:, 15:C:16]
@@ -266,10 +268,10 @@ def rank_program(g, core, T, topo):
         mm(4, C, *kk(7), T.qo[:], T.qos[:], ("qo", "kc7"))
         if t == 0:
             late_constants()
-        scan(T.dd[:], ps(4), T.k16[:], ("ps4", "k16"), "dd")
-        tt(T.key0[:], ps(4), T.ij[:], A.subtract, ("ps4", "ij"), "key0")
-        ts(T.nl[:], dv, -1.0 / 512, 287.0 - B16 / 512, A.mult, A.add, "dd", "nl")
-        ts(T.nf[:], dv, -1.0 / 512, 287.0 - B16 / 512, A.mult, A.add, "dd", "nf")
+        scan(T.dd[:], ps(4), T.k16[:], ("ps4", "k16"), D01)
+        tt(T.key0[:], ps(4), T.ij[:], A.subtract, ("ps4", "ij"), ("key0.0", "key0.1"))
+        ts(T.nl[:], dv, -1.0 / 512, 287.0 - B16 / 512, A.mult, A.add, D01, ("nl0", "nl1"))
+        ts(T.nf[:], dv, -1.0 / 512, 287.0 - B16 / 512, A.mult, A.add, D01, "nf")
         ts(T.ne[0:32, :], T.nf[0:32, :], T.mk[0:32, 0:1], None, A.mult, None, ("nf", "mk"), "ne")
         banks = ((5, 7), (6, 0), (1, 3), (2, 4))
         for k in range(4):
@@ -283,11 +285,14 @@ def rank_program(g, core, T, topo):
             return "w%d.%d.%d" % (ty, w, p)
 
         def rows(ty):
-            wt = side(ty)[0]
+            wt, d0 = side(ty)[0], 8 * C * ty
             for par in range(2):
                 k = 2 * ty + par
                 o = C * k
                 tt(T.rm[:, o:o + C], ps(banks[k][0]), T.hb[:], A.max, ("ps%d" % banks[k][0], "hb"), "rm%d" % k)
+            for par in range(2):
+                k = 2 * ty + par
+                o = C * k
                 op("v", lambda: V.transpose(T.tr[:, o:o + C], T.rm[:, o:o + C]), "rm%d" % k, "tr%d" % k)
             for w in range(2):
                 for par in range(2):
@@ -295,13 +300,13 @@ def rank_program(g, core, T, topo):
                     bw = banks[k][1]
                     for i in range(2):
                         b, z = (0, 1, 7, 8)[2 * w + i], 4 * C * w + 2 * par + i
-                        act(T.ds[:, z:4 * C * (w + 1):4], ps(bw), F.Identity, ("ps%d" % bw, "tr%d" % k), "ds%d.%d" % (w, 2 * par + i),
+                        act(T.ds[:, d0 + z:d0 + 4 * C * (w + 1):4], ps(bw), F.Identity, ("ps%d" % bw, "tr%d" % k), "ds%d.%d.%d" % (ty, w, 2 * par + i),
                             bias=T.tr[:, C * k + 32 * b:C * k + 32 * b + 1], scale=-1.0)
-                for st, lo, hi, s in (((1, 32, C, 1), (2, 0, 32, 1), (-2, 0, 32, -1)),
-                                      ((1, 0, 224, -1), (2, 224, 256, 1), (-2, 224, 256, -1), (1, 256, C, 1)))[w]:
-                    f = 4 * C * w + (st < 0)
-                    act(wt[:, 12 * C + f + 4 * lo:12 * C + 4 * C * w + 4 * hi:abs(st)], T.ds[:, f + 4 * lo:4 * C * w + 4 * hi:abs(st)], F.Sign,
-                        ["ds%d.%d" % (w, p) for p in range(4)] + ["f13", "f16"], [pl(ty, 3 + w, p) for p in range(4)], bias=col(13 if s > 0 else 16))
+            for w, st, lo, hi, s in ((0, 1, 32, C, 1), (0, 2, 0, 32, 1), (0, -2, 0, 32, -1),
+                                     (1, 1, 0, 224, -1), (1, 2, 224, 256, 1), (1, -2, 224, 256, -1), (1, 1, 256, C, 1)):
+                f = 4 * C * w + (st < 0)
+                act(wt[:, 12 * C + f + 4 * lo:12 * C + 4 * C * w + 4 * hi:abs(st)], T.ds[:, d0 + f + 4 * lo:d0 + 4 * C * w + 4 * hi:abs(st)], F.Sign,
+                    ["ds%d.%d.%d" % (ty, w, p) for p in range(4)] + ["f13", "f16"], [pl(ty, 3 + w, p) for p in range(4)], bias=col(13 if s > 0 else 16))
 
         def word(ty, w):
             wt, qn, pb = side(ty)
@@ -309,6 +314,8 @@ def rank_program(g, core, T, topo):
             c = (4, 4, 6, 5, 5)[w]
             qz(qc[:, C * w:C * w + C], qs[:, C * w:C * w + C], wt[:, 4 * C * w:4 * C * w + 4 * C], [pl(ty, w, p) for p in range(4)], qn + "%d" % w)
             mm(pb, C, *kk(c), qc[:, C * w:C * w + C], qs[:, C * w:C * w + C], (qn + "%d" % w, "kc%d" % c), w == 0, w == 4)
+
+        due = []
 
         def blocks(ty, par):
             wt = side(ty)[0]
@@ -322,7 +329,9 @@ def rank_program(g, core, T, topo):
                 z = 4 * C * w + p
                 ts(wt[:, z:z + 128 * b - 3:4], ps(bv, 32 * b), sc, None, A.is_lt, None, rd, pl(ty, w, p))
                 ts(wt[:, z + 128 * b:4 * C * (w + 1):4], T.ps[:, 512 * bv + 32 * b:512 * bv + C], sc, None, A.is_le, None, rd, pl(ty, w, p))
-                if par and (b % 2 or b == 6): word(ty, w)
+                while due:
+                    word(*due.pop())
+                if par and (b % 2 or b == 6): due.append((ty, w))
 
         rows(0)
         blocks(0, 0)
@@ -332,9 +341,10 @@ def rank_program(g, core, T, topo):
         word(0, 3)
         word(0, 4)
         blocks(1, 1)
-        scan(T.dd[:], ps(5), T.k16[:], ("ps5", "k16"), "dd")
-        ts(T.aw[:], dv, B16 + 64, None, A.add, None, "dd", "aw")
+        scan(T.dd[:], ps(5), T.k16[:], ("ps5", "k16"), D01)
+        word(*due.pop())
         word(1, 3)
+        ts(T.aw[:], dv, B16 + 64, None, A.add, None, D01, "aw")
         word(1, 4)
         op("v", lambda: V.tensor_copy(T.of[:].indirect(T.aw[:]), T.ij[:]), ("ij", "aw"), "of")
         if t == 0:
@@ -344,9 +354,12 @@ def rank_program(g, core, T, topo):
             last_constants()
         ts(T.bs[:], ps(1), 0.0625, -5.0, A.mult, A.add, "ps1", "bs")
         op("v", lambda: V.tensor_copy(T.cs[:].indirect(T.aw[:]), T.bs[:]), ("bs", "aw"), "cs")
-        ts(T.cd[:, 0:4 * C:4], T.cs[:], MAGIC, MAGIC, A.add, A.subtract, "cs", "cd0")
-        tt(T.cd[:, 1:4 * C:4], T.cs[:], T.cd[:, 0:4 * C:4], A.subtract, ("cs", "cd0"), "cd1")
-        qz(T.qc[:], T.qcs[:], T.cd[:], ("cd0", "cd1", "cdz"), "qc")
+        for h, (a, b) in enumerate(PARTS):
+            ts(T.cd[:, 4 * a:4 * b:4], T.cs[:, a:b], MAGIC, MAGIC, A.add, A.subtract, "cs", "cd0%d" % h)
+        for h, (a, b) in enumerate(PARTS):
+            tt(T.cd[:, 4 * a + 1:4 * b:4], T.cs[:, a:b], T.cd[:, 4 * a:4 * b:4], A.subtract, ("cs", "cd0%d" % h), "cd1%d" % h)
+        for h, (a, b) in enumerate(PARTS):
+            qz(T.qc[:, a:b], T.qcs[:, a:b], T.cd[:, 4 * a:4 * b], ("cd0%d" % h, "cd1%d" % h, "cdz"), "qc")
         bb = (0, 2, 3, 4, 6, 7, 0, 2)
 
         def table(k):
@@ -364,28 +377,69 @@ def rank_program(g, core, T, topo):
         keep(1)
         keys = ((T.key0, "key0"), (T.key1, "key1"))
 
-        def grow(k):
-            (a, an), (b, bn) = keys[k % 2], keys[1 - k % 2]
-            op("v", lambda: V.tensor_tensor(b[:], T.cw[:, C * k:C * k + C].indirect(T.nl[:]), a[:], A.add), ("cw%d" % k, "nl", an), bn)
+        def grow(k, h):
+            (x, xk), (y, yk) = keys[k % 2], keys[1 - k % 2]
+            a, b = PARTS[h]
+            op("v", lambda: V.tensor_tensor(y[:, a:b], T.cw[:, C * k:C * k + C].indirect(T.nl[:, a // 16:b // 16]), x[:, a:b], A.add),
+               ("cw%d" % k, "nl%d" % h, "%s.%d" % (xk, h)), "%s.%d" % (yk, h))
 
-        grow(0)
+        def turns(h):
+            a, b = PARTS[h]
+            ts(T.nl[:, a // 16:b // 16], dv[:, a // 16:b // 16], B16 + 48, None, A.add, None, "%s%d" % (dn, h), "nl%d" % h)
+
         fb = (3, 4, 6, 7)
+        dn = "dd"
+        zc, zs = T["zc%d" % t], T["zs%d" % t]
+
+        def z_list(h, i):
+            s = slice(PARTS[h][0] // 16, PARTS[h][1] // 16)
+            if i == 0: ts(T.no[96:128, s], dv[96:128, s], B16 + 48, T.mk[96:128, 1:2], A.add, A.mult, (dn + "%d" % h, "mk"), "no")
+            if i == 1: tt(T.nf[:, s], T.ne[:, s], T.no[:, s], A.add, ("ne", "no"), "nf%d" % h)
+            if i == 2: cp(T.nz[:, s], T.nf[:, s], "nf%d" % h, "nz%d" % h)
+
+        def z_part(b, h, v):
+            a, e = PARTS[h]
+            o, i = zt[:, 4 * a + b:4 * e:4], T.fs[:, C * b:C * b + C].indirect(T.nz[:, a // 16:e // 16])
+            rd, wr = ("fs%d" % b, "nz%d" % h), "zt%d.%d" % (b, h)
+            if v: cp(o, i, rd, wr)
+            else: op("s", lambda: S.activation(o, i, F.Copy), rd, wr)
+
+        def z_codes(h):
+            a, b = PARTS[h]
+            qz(zc[:, a:b], zs[:, a:b], zt[:, 4 * a:4 * b], ["zt%d.%d" % (i, h) for i in range(4)], "zc")
+
         for k in range(1, 8):
             kr, kn = keys[k % 2]
-            scan(T.col[:], kr[:], T.k96[:], (kn, "k96"), "col")
-            act(ct[:, 2:4 * C:4], kr[:], F.Sign, (kn, "col"), "ct2", bias=T.col[:, 287:288], scale=-1.0)
-            for p in range(2):
-                ts(ct[:, p:4 * C:4], kr[:], -B96, T.col[:, 96 * p + 95:96 * p + 96], A.add, A.is_lt, (kn, "col"), "ct%d" % p)
-            for h in range(2):
-                a, b = (0, H, C)[h:h + 2]
-                qz(T.qt[:, a:b], T.qts[:, a:b], ct[:, 4 * a:4 * b], ("ct0", "ct1", "ct2", "ctz"), "qt%d" % h)
+            k0, k1 = kn + ".0", kn + ".1"
+
+            def pick(b, rd):
+                scan(T.col[:, 96 * b:96 * b + 96], kr[:, 96 * b:96 * b + 96], T.k96[:, 96 * b:96 * b + 96], rd + ("k96",), "col%d" % b)
+
+            def less(b, h):
+                a, e = PARTS[h]
+                ts(ct[:, 4 * a + b:4 * e:4], kr[:, a:e], -B96, T.col[:, 96 * b + 95:96 * b + 96], A.add, A.is_lt, ((k0, k1)[h], "col%d" % b), "ct%d.%d" % (b, h))
+
+            grow(k - 1, 0)
+            if k > 1: turns(1)
+            pick(0, (k0,))
+            grow(k - 1, 1)
+            less(0, 0)
+            pick(2, (k1,))
+            for h, (a, b) in enumerate(PARTS):
+                act(ct[:, 4 * a + 2:4 * b:4], kr[:, a:b], F.Sign, ((k0, k1)[h], "col2"), "ct2.%d" % h, bias=T.col[:, 287:288], scale=-1.0)
+            pick(1, (k0, k1))
+            less(0, 1)
+            less(1, 0)
+            less(1, 1)
+            for h, (a, b) in enumerate(PARTS):
+                qz(T.qt[:, a:b], T.qts[:, a:b], ct[:, 4 * a:4 * b], ["ct%d.%d" % (i, h) for i in range(3)] + ["ctz"], "qt%d" % h)
                 mm((5, 1)[h], b - a, *kk(8), T.qt[:, a:b], T.qts[:, a:b], ("qt%d" % h, "kc8"))
             dx, dn = ((T.dd, "dd"), (T.de, "de"))[k % 2]
             dv = dx[:, 15:C:16]
-            scan(dx[:, 0:H], ps(5, H), T.k16[:, 0:H], ("ps5", "k16"), dn)
             if t == 0:
                 for i in {1: (11, 12), 2: (13, 14, 0), 3: (15, 16, 1), 4: (2, 3)}.get(k, ()):
                     kz(i)
+            scan(dx[:, 0:H], ps(5, H), T.k16[:, 0:H], ("ps5", "k16"), dn + "0")
             if k <= 3:
                 if t == 0:
                     table(2 * k)
@@ -402,35 +456,43 @@ def rank_program(g, core, T, topo):
             if k in (6, 7):
                 for b in (2 * k - 12, 2 * k - 11):
                     op("s", lambda: S.activation(T.fs[:, C * b:C * b + C], T.ff[:, C * b:C * b + C].indirect(T.ow[:]), F.Copy), ("ff%d" % b, "ow"), "fs%d" % b)
-            scan(dx[:, H:C], ps(1, C - H), T.k16[:, H:C], ("ps1", "k16"), dn)
-            if k < 7 or t:
-                ts(T.nl[:], dv, B16 + 48, None, A.add, None, dn, "nl")
-            if k < 7:
-                grow(k)
+            if k < 7: turns(0)
+            else:
+                for i in range(3):
+                    z_list(0, i)
+            scan(dx[:, H:C], ps(1, C - H), T.k16[:, H:C], ("ps1", "k16"), dn + "1")
             p0, m = 32 * (k // 2), k % 2
             p1 = p0 + 32
             nb, nn = ((T.ne, "ne"), (T.no, "no"))[m]
-            if k < 7: act(nb[p0:p1, :], dv[p0:p1, :], F.Identity, (dn, "mk"), nn, bias=T.mk[p0:p1, 2 + m:3 + m], scale=T.mk[p0:p1, m:m + 1])
-            else: ts(nb[p0:p1, :], dv[p0:p1, :], B16 + 48, T.mk[p0:p1, 1:2], A.add, A.mult, (dn, "mk"), nn)
-        tt(T.nf[:], T.ne[:], T.no[:], A.add, ("ne", "no"), "nf")
-        cp(T.nz[:], T.nf[:], "nf", "nz")
+            if k < 7: act(nb[p0:p1, :], dv[p0:p1, :], F.Identity, (dn + "0", dn + "1", "mk"), nn, bias=T.mk[p0:p1, 2 + m:3 + m], scale=T.mk[p0:p1, m:m + 1])
+        z_part(0, 0, True)
+        z_part(3, 0, False)
+        z_list(1, 0)
+        z_part(1, 0, True)
+        z_list(1, 1)
+        z_part(2, 0, True)
+        z_list(1, 2)
+        z_codes(0)
+        z_part(0, 1, True)
+        z_part(2, 1, False)
+        z_part(3, 1, False)
+        z_part(1, 1, True)
+        z_codes(1)
+        if t:
+            turns(0)
+            turns(1)
         dv = T.dd[:, 15:C:16]
-        zc, zs = T["zc%d" % t], T["zs%d" % t]
-        for b in (0, 1):
-            cp(T.zt[:, b:4 * C:4], T.fs[:, C * b:C * b + C].indirect(T.nz[:]), ("fs%d" % b, "nz"), "zt%d" % b)
-        for b in (2, 3):
-            op("s", lambda: S.activation(T.zt[:, b:4 * C:4], T.fs[:, C * b:C * b + C].indirect(T.nz[:]), F.Copy), ("fs%d" % b, "nz"), "zt%d" % b)
-        qz(zc[:], zs[:], T.zt[:], ["zt%d" % b for b in range(4)], "zc")
         for b in range(4):
             for h in range(2):
                 w = 128 * (b + 4 * h)
                 mm(2 * b + h, C, T.wk[:, w:w + 128], T.wp[:, w:w + 128], zc[:], zs[:], ("zc", "wk", "wp"))
-        op("v", lambda: V.tensor_copy(T.nv[:].indirect(T.nz[:]), T.ij[:]), ("ij", "nz"), "nv")
+        op("v", lambda: V.tensor_copy(T.nv[:].indirect(T.nz[:]), T.ij[:]), ("ij", "nz0", "nz1"), "nv")
         cp(T.kr[:], T.nv[:].indirect(T.aw[:]), ("nv", "aw"), "kr")
         if t:
-            grow(7)
-        scan(T.dd[:], T.kr[:], T.k16[:], ("kr", "k16"), "dd")
-        ts(T.kw[:], dv, B16, None, A.add, None, "dd", "kw")
+            grow(7, 0)
+            grow(7, 1)
+        scan(T.dd[:], T.kr[:], T.k16[:], ("kr", "k16"), D01)
+        ts(T.kw[:], dv, B16, None, A.add, None, D01, "kw")
 
         def largest(b):
             act(T.y1[:, C * b:C * b + C], ps(2 * b), F.Copy, "ps%d" % (2 * b), "y1%d" % b)
@@ -455,7 +517,7 @@ def rank_program(g, core, T, topo):
         for b in range(4):
             mm(b, C, *kk(b), xc[:], xs[:], xn + ("kc%d" % b,), True, False)
         if t == 1:
-            tt(T.to[0:1, :], T.key0[0:1, :], T.ij[0:1, :], A.add, ("key0", "ij"), "to")
+            tt(T.to[0:1, :], T.key0[0:1, :], T.ij[0:1, :], A.add, ("key0.0", "key0.1", "ij"), "to")
             ts(T.to[0:1, :], T.to[0:1, :], 1.0 / 512, 1152.0, A.mult, A.add, "to", "to")
             ld("y", T.tot[:], T.to[0:1, :], "tot", "to")
             qz(T.vq[:], T.vs[:], T.vt[:], "vt", "vq")

from concourse.mybir import dt, AluOpType as A, ActivationFunctionType as F

C = 288
H = 160
PARTS = ((0, H), (H, C))
KW = 512
B16, B96 = 2.0 ** 18, 2.0 ** 21
BIG, TINY, MAGIC = 1e29, 2.0 ** -119, 1.5 * 2.0 ** 23
NK = 17

MXC, PL = "float8_e4m3fn_x4", "uint8"
SCRATCH = {}


def _buf(n, cols, d):
    SCRATCH[n] = ("psum" if n == "ps" else "sbuf", [128, cols], d)


_buf("ps", 4096, "float32")
for _t in range(3):
    _buf("xt%d" % _t, 4 * C, "bfloat16")
    _buf("xc%d" % _t, C, MXC)
    _buf("xs%d" % _t, C, PL)
for _t in range(2):
    for _n in ("l", "z", "q", "b"):
        _buf(_n + "c%d" % _t, C, MXC)
        _buf(_n + "s%d" % _t, C, PL)
for _n, _c, _d in (("wk", 1024, MXC), ("wp", 1024, PL), ("ut", 512, "bfloat16"), ("vt", 512, "bfloat16"), ("uq", 128, MXC), ("us", 128, PL),
                   ("vq", 128, MXC), ("vs", 128, PL), ("up", 640, MXC), ("ups", 640, PL), ("kt", NK * 512, "bfloat16"), ("kc", NK * 128, MXC),
                   ("ks", NK * 128, PL), ("tm2", 512, "bfloat16"), ("ui", 40, "int32"), ("ul", 40, "uint16"), ("pi", 2, "int32"), ("pj", 4, "int32"),
                   ("fc", 20, "float32"), ("mk", 4, "float32"), ("bcm", 8, "float32"), ("ij", C, "float32"), ("rowx", C, "float32"),
                   ("row16", C, "float32"), ("row32", C, "float32"), ("row96", C, "float32"), ("rowog", 128, "float32"), ("hown", C, "float32"),
                   ("hb", C, "float32"), ("k16", C, "float32"), ("k96", C, "float32"), ("t1", C, "float32"), ("t2", C, "float32"),
                   ("t3", C, "float32"), ("t4", C, "float32"), ("wo", 4 * C, "bfloat16"), ("qo", C, MXC), ("qos", C, PL), ("om", C, "float32"),
                   ("wa", 20 * C, "bfloat16"), ("wb", 20 * C, "bfloat16"), ("qa", 5 * C, MXC), ("qas", 5 * C, PL), ("qb", 5 * C, MXC),
                   ("qbs", 5 * C, PL), ("rm", 4 * C, "float32"), ("tr", 4 * C, "float32"), ("ds", 16 * C, "float32"), ("dd", C, "float32"),
                   ("de", C, "float32"), ("key0", C, "float32"), ("key1", C, "float32"), ("col", C, "float32"), ("nl", 18, "uint16"),
                   ("nf", 18, "float32"), ("ne", 18, "float32"), ("no", 18, "float32"), ("nz", 18, "uint16"), ("aw", 18, "uint16"),
                   ("ow", 18, "uint16"), ("kw", 18, "uint16"), ("bs", C, "float32"), ("cs", C, "float32"), ("of", C, "float32"),
                   ("nv", C, "float32"), ("kr", C, "float32"), ("cd", 4 * C, "bfloat16"), ("qc", C, MXC), ("qcs", C, PL), ("cw", 8 * C, "float32"),
                   ("ct", 4 * C, "bfloat16"), ("qt", C, MXC), ("qts", C, PL), ("ff", 4 * C, "bfloat16"), ("fs", 4 * C, "bfloat16"),
                   ("zt", 4 * C, "bfloat16"), ("y1", 4 * C, "float32"), ("ym", 4 * C, "bfloat16"), ("yt", 4 * C, "bfloat16"),
                   ("yo", C, "float32"), ("to", C, "float32")):
    _buf(_n, _c, _d)
DMAS = ["d%d" % i for i in range(20)]
SEMAPHORES = ["cv", "cs", "ct", "cg", "sent", "ax0", "ax1", "ay0", "ay1"] + DMAS


def rank_program(g, core, T, topo):
    rank = T.rank_of(core)
    if rank is None:
        return
    Q = {"g": g, "v": g.vector, "s": g.scalar, "t": g.tensor, "y": g.sync}
    clk = {k: {} for k in Q}
    cnt = {k: 0 for k in Q}
    last, readers, ndma, sent = {}, {}, [0], [0]

    def waits(q, toks):
        for s, v, c, _ in sorted(toks, key=lambda k: -len(k[2])):
            if clk[q].get(s, 0) < v:
                Q[q].wait_ge(T.sem[s], max(k[1] for k in toks if k[0] == s))
                for k in toks:
                    if k[0] == s:
                        for a, b in k[2].items():
                            if clk[q].get(a, 0) < b: clk[q][a] = b

    def op(q, fn, rd=(), wr=(), dma=False):
        rd = (rd,) if isinstance(rd, str) else rd
        wr = (wr,) if isinstance(wr, str) else wr
        me = "dma" if dma else q
        toks = []
        for k in rd:
            if k in last: toks.append(last[k])
            if k[:2] == "ps": toks += [w for w in readers.get(k, {}).values() if w[3] != me]
        for k in wr:
            if k in last and last[k][3] != q: toks.append(last[k])
            toks += list(readers.get(k, {}).values())
        waits(q, toks)
        ins = fn()
        if dma:
            s, v = DMAS[ndma[0]], 16
            ndma[0] += 1
        else:
            cnt[q] += 1
            s, v = "c" + q, cnt[q]
        ins.then_inc(T.sem[s], 16 if dma else 1)
        c = dict(clk[q])
        c[s] = v
        tok = (s, v, c, me)
        for k in rd:
            readers.setdefault(k, {})[s] = tok
        for k in wr:
            last[k] = tok
            readers[k] = {}

    V, S = g.vector, g.scalar

    def ts(out, i, s1, s2, o0, o1, rd, wr):
        if o1 is None: op("v", lambda: V.tensor_scalar(out, i, s1, None, o0), rd, wr)
        else: op("v", lambda: V.tensor_scalar(out, i, s1, s2, o0, o1), rd, wr)

    def tt(out, a, b, o, rd, wr):
        op("v", lambda: V.tensor_tensor(out, a, b, o), rd, wr)

    def cp(out, i, rd, wr):
        op("v", lambda: V.tensor_copy(out, i), rd, wr)

    def ms(ap, c, wr):
        op("v", lambda: V.memset(ap, c), (), wr)

    def act(out, i, f, rd, wr, bias=0.0, scale=1.0):
        op("s", lambda: S.activation(out, i, f, bias=bias, scale=scale), rd, wr)

    def qz(c, s, i, rd, wr):
        op("v", lambda: V.quantize_mx(c, s, i), rd, wr)

    def iota(out, pat, base, cm, wr, flag=True):
        op("g", lambda: g.iota(out, pat, base, cm, allow_small_or_imprecise_dtypes=flag), (), wr)

    def ld(q, out, i, wr, rd=()):
        op(q, lambda: Q[q].dma_start(out, i), rd, wr, dma=True)

    def ps(b, n=C):
        return T.ps[:, 512 * b:512 * b + n]

    def mm(b, n, lc, ls, rc, rs, rd, start=True, stop=True):
        op("t", lambda: g.tensor.matmul_mx(ps(b, n), lc, ls, rc, rs, start, stop), rd, "ps%d" % b)

    def kk(i):
        return T.kc[:, 128 * i:128 * i + 128], T.ks[:, 128 * i:128 * i + 128]

    def kz(k):
        qz(*kk(k), T.kt[:, k * KW:(k + 1) * KW], "kt%d" % k, "kc%d" % k)

    def scan(out, i, k, rd, wr):
        op("v", lambda: V.tensor_tensor_scan(out, i, k, -4.0 * B96, A.max, A.add), rd, wr)

    def send(src, dst, sem, peer):
        waits("g", [last[k] for k in src])
        rid, pid = topo.addr(peer, core)
        m = topo.mask(core, peer)
        g.remote_dma(T[dst[0]][:].bitcast(dt.uint8), T[src[0]][:].bitcast(dt.uint8), T.sem[sem], T.sem.sent, pid, rid, m)
        g.remote_dma(T[dst[1]][:], T[src[1]][:], T.sem[sem], T.sem.sent, pid, rid, m)
        n = 2 * len(topo.engines(core, peer))
        sent[0] += n
        for k in dst:
            last[k] = (sem, n, {sem: n}, "r")

    peers = [T.cores[rank ^ (1 << t)] for t in range(2)]

    ld("y", T.xt0[:], T.x[:], "xt0")
    ld("s", T.ut[:], T.u[:], "ut")
    ld("y", T.wk[:].bitcast(dt.uint8), T.wc[:], "wk")
    ld("y", T.wp[:], T.ws[:], "wp")
    ld("y", T.vt[:], T.v[:], "vt")

    iota(T.pi[:, 0:1], [[1, 1]], 0, 1, "pi", False)
    iota(T.ui[:, 0:16], [[16, 2], [32, 4], [0, 2]], 0, 0, "ui", False)
    iota(T.ui[:, 16:32], [[16, 2], [32, 4], [0, 2]], 1, 0, "ui", False)
    iota(T.rowx[:, 0:256], [[0, 2], [1, 128]], 0, 0, "rowx")
    iota(T.rowx[:, 256:C], [[1, 32]], 96, 0, "rowx")
    iota(T.row16[:], [[0, 18], [1, 16]], 0, 0, "row16")
    iota(T.rowog[:], [[1, 8], [0, 16]], 0, 0, "rowog")
    iota(T.ij[:], [[1, C]], 0, 0, "ij")

    def col(i):
        return T.fc[:, i:i + 1]

    def picker(row, rn, c0, c1, step):
        for t, n, c in ((T.t1, "t1", c0), (T.t2, "t2", c1)):
            act(t[:], row, F.Abs, (rn, "f%d" % c), n, bias=col(c))
            act(t[:], t[:], F.Relu, n, n, bias=col(14 if step == B16 else 15), scale=-step)

    for i, x in ((13, TINY), (16, -TINY), (14, B16), (15, B96)):
        ms(col(i), x, "f%d" % i)
    ms(T.ui[:, 32:40], 0, "uz")
    cp(col(0), T.pi[:, 0:1], "pi", "f0")
    for i, (o, k) in enumerate(((A.bitwise_and, 15), (A.bitwise_and, 31), (A.arith_shift_right, 4), (A.arith_shift_right, 5))):
        ts(T.pj[:, i:i + 1], T.pi[:, 0:1], k, None, o, None, "pi", "pj")
    cp(T.fc[:, 1:5], T.pj[:], "pj", "f1")
    for i, j, a, b in ((10, 0, -BIG, -0.5 * BIG), (5, 1, -1.0, 0.0), (6, 1, -1.0, 1.0), (7, 2, BIG, -0.5 * BIG), (8, 0, -1.0, 0.0),
                       (9, 0, -1.0, 1.0), (11, 4, 2.0, 0.0), (12, 4, 2.0, 1.0)):
        ts(col(i), col(j), a, b, A.mult, A.add, ("f0", "f1"), "f%d" % i)
    act(T.hown[:], T.rowx[:], F.Identity, ("rowx", "f10"), "hown", bias=col(10), scale=BIG)
    picker(T.row16[:], "row16", 5, 6, B16)
    for w, (lo, hi, val) in ((0, (0, 128, 512.0)), (1, (0, 128, 512.0)), (3, (0, 128, -512.0)), (2, (0, 96, 0.0)), (2, (96, 128, 512.0))):
        ms(T.kt[lo:hi, 7 * KW + w:8 * KW:4], val, "kt7")
    cp(T.ul[:], T.ui[:], ("ui", "uz"), "ul")
    qz(T.uq[:], T.us[:], T.ut[:], "ut", ("uq", "us"))

    def upick(i):
        a, b = 128 * i, 128 * i + 128
        off = T.ul[:, 8 * i:8 * i + 8]
        op("v", lambda: V.tensor_copy(T.up[:, a:b].bitcast(dt.uint32), T.uq[:, 0:128].bitcast(dt.uint32).indirect(off)), ("uq", "ul"), "up%d" % i)
        op("s", lambda: S.activation(T.ups[:, a:b], T.us[:, 0:128].indirect(off), F.Copy), ("us", "ul"), "ups%d" % i)

    upick(4)
    qz(T.xc0[:], T.xs0[:], T.xt0[:], "xt0", ("xc0", "xs0"))
    send(("xc0", "xs0"), ("lc0", "ls0"), "ax0", peers[0])
    iota(T.row32[:], [[0, 9], [1, 32]], 0, 0, "row32")
    iota(T.row96[:], [[0, 3], [1, 96]], 0, 0, "row96")
    for t in range(4):
        iota(T.tm2[:, t:512:4], [[0, 128]], 8192 if t < 2 else 0, 0, "tm2")
    for t in range(2, 4):
        iota(T.cd[:, t:4 * C:4], [[0, C]], 0, 0, "cdz")
    iota(T.ct[:, 3:4 * C:4], [[0, C]], 0, 0, "ctz")
    for k in range(4):
        iota(T.kt[:, k * KW:(k + 1) * KW], [[0, KW]], 0, 0, "kt%d" % k)
    kz(7)
    tt(T.k16[:], T.t1[:], T.t2[:], A.subtract, ("t1", "t2"), "k16")
    ts(T.k16[:, 15:C:16], T.k16[:, 15:C:16], -2.0 * B16, None, A.add, None, "k16", "k16")
    ts(T.t3[:, 0:128], T.rowog[:], col(11), None, A.is_equal, None, ("rowog", "f11"), "t3")
    ts(T.t4[:, 0:128], T.rowog[:], col(12), None, A.is_equal, None, ("rowog", "f12"), "t4")
    for i in range(4):
        upick(i)
    for k, w in ((4, (1.0, 1.0)), (5, (0.5, 0.5)), (6, (1.0, -1.0))):
        for t in range(4):
            src, n = (T.t3, "t3") if t < 2 else (T.t4, "t4")
            act(T.kt[:, k * KW + t:(k + 1) * KW:4], src[:, 0:128], F.Copy, n, "kt%d" % k, scale=w[t % 2])
    act(T.hb[:], T.row32[:], F.Identity, ("row32", "f7"), "hb", bias=col(7), scale=-BIG)

    def spread(ks):
        for k in ks:
            act(T.kt[:, (9 + k) * KW:(10 + k) * KW], T.tm2[:], F.Copy, ("tm2", "bcm"), "kt%d" % (9 + k), scale=T.bcm[:, k:k + 1])

    def late_constants():
        for m in range(2):
            ts(T.mk[:, m:m + 1], col(2), 15.5, None, (A.is_lt, A.is_gt)[m], None, "f1", "mk")
            ts(T.mk[:, m + 2:m + 3], col(2), 15.5, B16 + 48, (A.is_lt, A.is_gt)[m], A.mult, "f1", "mk")
        ts(T.bcm[:], T.ij[:, 0:8], 16.0, col(0), A.mult, A.is_equal, ("ij", "f0"), "bcm")
        for t, w in enumerate((1.0, 1.0, 0.5, 0.0)):
            ms(T.kt[0:96, 8 * KW + t:9 * KW:4], w, "kt8")
        ms(T.kt[96:128, 8 * KW:9 * KW], 0.0, "kt8")
        picker(T.row96[:], "row96", 8, 9, B96)
        spread((0, 1))
        for k in (4, 5, 6):
            kz(k)

    def last_constants():
        for i in (9, 10, 8):
            kz(i)
        tt(T.k96[:], T.t1[:], T.t2[:], A.subtract, ("t1", "t2"), "k96")
        ts(T.k96[:, 95:192:96], T.k96[:, 95:192:96], -2.0 * B96, None, A.add, None, "k96", "k96")
        ts(T.k96[:, 287:C], T.k96[:, 287:C], -B96 - 0.5, None, A.add, None, "k96", "k96")

    wo, ct, zt = T.wo, T.ct, T.zt
    D01 = ("dd0", "dd1")
    for t in range(2):
        peer = peers[t]
        dv = T.dd[:, 15:C:16]
        xc, xs = T["xc%d" % t], T["xs%d" % t]
        xn = ("xc%d" % t, "xs%d" % t)
        lc, ls = T["lc%d" % t], T["ls%d" % t]
        ln = ("lc%d" % t, "ls%d" % t)
        m0 = (0, 128, 160)
        mm(3, C, T.up[:, 512:640], T.ups[:, 512:640], xc[:], xs[:], xn + ("up4", "ups4"))
        for q in range(3):
            mm(q, 128, xc[:, m0[q]:m0[q] + 128], xs[:, m0[q]:m0[q] + 128], T.uq[:], T.us[:], xn + ("uq", "us"))
        tt(T.om[:], ps(3), T.hown[:], A.max, ("ps3", "hown"), "om")
        for q in range(3):
            sc = T.ps[:, 512 * q:512 * q + 1]
            rq = ("ps3", "ps%d" % q)
            e0, e1 = 128 * q, min(128 * q + 128, C)
            if e0: ts(wo[:, q:4 * e0:4], ps(3, e0), sc, None, A.is_lt, None, rq, "wo")
            ts(wo[:, 4 * e0 + q:4 * C:4], T.ps[:, 1536 + e0:1536 + C], sc, None, A.is_le, None, rq, "wo")
            ts(wo[:, 4 * e0 + 3:4 * e1:4], T.om[:, e0:e1], sc, None, A.is_equal, None, ("om", rq[1]), "wo")
        qz(T.qo[:], T.qos[:], wo[:], "wo", "qo")
        mm(4, C, *kk(7), T.qo[:], T.qos[:], ("qo", "kc7"))
        if t == 0:
            late_constants()
        scan(T.dd[:], ps(4), T.k16[:], ("ps4", "k16"), D01)
        tt(T.key0[:], ps(4), T.ij[:], A.subtract, ("ps4", "ij"), ("key0.0", "key0.1"))
        ts(T.nl[:], dv, -1.0 / 512, 287.0 - B16 / 512, A.mult, A.add, D01, ("nl0", "nl1"))
        ts(T.nf[:], dv, -1.0 / 512, 287.0 - B16 / 512, A.mult, A.add, D01, "nf")
        ts(T.ne[0:32, :], T.nf[0:32, :], T.mk[0:32, 0:1], None, A.mult, None, ("nf", "mk"), "ne")
        banks = ((5, 7), (6, 0), (1, 3), (2, 4))
        for k in range(4):
            for b in banks[k]:
                mm(b, C, T.up[:, 128 * k:128 * k + 128], T.ups[:, 128 * k:128 * k + 128], lc[:], ls[:], ln + ("up%d" % k, "ups%d" % k))

        def side(ty):
            return (T.wa, "qa", 5) if ty == 0 else (T.wb, "qb", 1)

        def pl(ty, w, p):
            return "w%d.%d.%d" % (ty, w, p)

        def rows(ty):
            wt, d0 = side(ty)[0], 8 * C * ty
            for par in range(2):
                k = 2 * ty + par
                o = C * k
                tt(T.rm[:, o:o + C], ps(banks[k][0]), T.hb[:], A.max, ("ps%d" % banks[k][0], "hb"), "rm%d" % k)
            for par in range(2):
                k = 2 * ty + par
                o = C * k
                op("v", lambda: V.transpose(T.tr[:, o:o + C], T.rm[:, o:o + C]), "rm%d" % k, "tr%d" % k)
            for w in range(2):
                for par in range(2):
                    k = 2 * ty + par
                    bw = banks[k][1]
                    for i in range(2):
                        b, z = (0, 1, 7, 8)[2 * w + i], 4 * C * w + 2 * par + i
                        act(T.ds[:, d0 + z:d0 + 4 * C * (w + 1):4], ps(bw), F.Identity, ("ps%d" % bw, "tr%d" % k), "ds%d.%d.%d" % (ty, w, 2 * par + i),
                            bias=T.tr[:, C * k + 32 * b:C * k + 32 * b + 1], scale=-1.0)
            for w, st, lo, hi, s in ((0, 1, 32, C, 1), (0, 2, 0, 32, 1), (0, -2, 0, 32, -1),
                                     (1, 1, 0, 224, -1), (1, 2, 224, 256, 1), (1, -2, 224, 256, -1), (1, 1, 256, C, 1)):
                f = 4 * C * w + (st < 0)
                act(wt[:, 12 * C + f + 4 * lo:12 * C + 4 * C * w + 4 * hi:abs(st)], T.ds[:, d0 + f + 4 * lo:d0 + 4 * C * w + 4 * hi:abs(st)], F.Sign,
                    ["ds%d.%d.%d" % (ty, w, p) for p in range(4)] + ["f13", "f16"], [pl(ty, 3 + w, p) for p in range(4)], bias=col(13 if s > 0 else 16))

        def word(ty, w):
            wt, qn, pb = side(ty)
            qc, qs = T[qn], T[qn + "s"]
            c = (4, 4, 6, 5, 5)[w]
            qz(qc[:, C * w:C * w + C], qs[:, C * w:C * w + C], wt[:, 4 * C * w:4 * C * w + 4 * C], [pl(ty, w, p) for p in range(4)], qn + "%d" % w)
            mm(pb, C, *kk(c), qc[:, C * w:C * w + C], qs[:, C * w:C * w + C], (qn + "%d" % w, "kc%d" % c), w == 0, w == 4)

        due = []

        def blocks(ty, par):
            wt = side(ty)[0]
            k = 2 * ty + par
            bv = banks[k][0]
            rd, o = ("ps%d" % bv, "tr%d" % k), C * k
            tt(wt[:, 8 * C + 2 * par + 1:12 * C:4], ps(bv), T.tr[:, o:o + C], A.is_equal, rd, pl(ty, 2, 2 * par + 1))
            for b in range(2, 7):
                w, p = (b - 2) // 2, 2 * par + b % 2
                sc = T.tr[:, o + 32 * b:o + 32 * b + 1]
                z = 4 * C * w + p
                ts(wt[:, z:z + 128 * b - 3:4], ps(bv, 32 * b), sc, None, A.is_lt, None, rd, pl(ty, w, p))
                ts(wt[:, z + 128 * b:4 * C * (w + 1):4], T.ps[:, 512 * bv + 32 * b:512 * bv + C], sc, None, A.is_le, None, rd, pl(ty, w, p))
                while due:
                    word(*due.pop())
                if par and (b % 2 or b == 6): due.append((ty, w))

        rows(0)
        blocks(0, 0)
        rows(1)
        blocks(0, 1)
        blocks(1, 0)
        word(0, 3)
        word(0, 4)
        blocks(1, 1)
        scan(T.dd[:], ps(5), T.k16[:], ("ps5", "k16"), D01)
        word(*due.pop())
        word(1, 3)
        ts(T.aw[:], dv, B16 + 64, None, A.add, None, D01, "aw")
        word(1, 4)
        op("v", lambda: V.tensor_copy(T.of[:].indirect(T.aw[:]), T.ij[:]), ("ij", "aw"), "of")
        if t == 0:
            spread(range(2, 8))
            for k in range(4):
                ts(T.kt[:, k * KW + k:(k + 1) * KW:4], T.ij[:, 0:128], col(0), None, A.is_equal, None, ("ij", "f0"), "kt%d" % k)
            last_constants()
        ts(T.bs[:], ps(1), 0.0625, -5.0, A.mult, A.add, "ps1", "bs")
        op("v", lambda: V.tensor_copy(T.cs[:].indirect(T.aw[:]), T.bs[:]), ("bs", "aw"), "cs")
        for h, (a, b) in enumerate(PARTS):
            ts(T.cd[:, 4 * a:4 * b:4], T.cs[:, a:b], MAGIC, MAGIC, A.add, A.subtract, "cs", "cd0%d" % h)
        for h, (a, b) in enumerate(PARTS):
            tt(T.cd[:, 4 * a + 1:4 * b:4], T.cs[:, a:b], T.cd[:, 4 * a:4 * b:4], A.subtract, ("cs", "cd0%d" % h), "cd1%d" % h)
        for h, (a, b) in enumerate(PARTS):
            qz(T.qc[:, a:b], T.qcs[:, a:b], T.cd[:, 4 * a:4 * b], ("cd0%d" % h, "cd1%d" % h, "cdz"), "qc")
        bb = (0, 2, 3, 4, 6, 7, 0, 2)

        def table(k):
            mm(bb[k], C, *kk(9 + k), T.qc[:], T.qcs[:], ("qc", "kc%d" % (9 + k)))

        def keep(k):
            if k: act(T.cw[:, C * k:C * k + C], ps(bb[k]), F.Copy, "ps%d" % bb[k], "cw%d" % k)
            else: cp(T.cw[:, 0:C], ps(bb[0]), "ps%d" % bb[0], "cw0")

        for k in range(2 if t == 0 else 6):
            table(k)
        scan(T.kr[:], T.of[:], T.k16[:], ("of", "k16"), "kr")
        ts(T.ow[:], T.kr[:, 15:C:16], B16, None, A.add, None, "kr", "ow")
        keep(0)
        keep(1)
        keys = ((T.key0, "key0"), (T.key1, "key1"))

        def grow(k, h):
            (x, xk), (y, yk) = keys[k % 2], keys[1 - k % 2]
            a, b = PARTS[h]
            op("v", lambda: V.tensor_tensor(y[:, a:b], T.cw[:, C * k:C * k + C].indirect(T.nl[:, a // 16:b // 16]), x[:, a:b], A.add),
               ("cw%d" % k, "nl%d" % h, "%s.%d" % (xk, h)), "%s.%d" % (yk, h))

        def turns(h):
            a, b = PARTS[h]
            ts(T.nl[:, a // 16:b // 16], dv[:, a // 16:b // 16], B16 + 48, None, A.add, None, "%s%d" % (dn, h), "nl%d" % h)

        fb = (3, 4, 6, 7)
        dn = "dd"
        zc, zs = T["zc%d" % t], T["zs%d" % t]

        def z_list(h, i):
            s = slice(PARTS[h][0] // 16, PARTS[h][1] // 16)
            if i == 0: ts(T.no[96:128, s], dv[96:128, s], B16 + 48, T.mk[96:128, 1:2], A.add, A.mult, (dn + "%d" % h, "mk"), "no")
            if i == 1: tt(T.nf[:, s], T.ne[:, s], T.no[:, s], A.add, ("ne", "no"), "nf%d" % h)
            if i == 2: cp(T.nz[:, s], T.nf[:, s], "nf%d" % h, "nz%d" % h)

        def z_part(b, h, v):
            a, e = PARTS[h]
            o, i = zt[:, 4 * a + b:4 * e:4], T.fs[:, C * b:C * b + C].indirect(T.nz[:, a // 16:e // 16])
            rd, wr = ("fs%d" % b, "nz%d" % h), "zt%d.%d" % (b, h)
            if v: cp(o, i, rd, wr)
            else: op("s", lambda: S.activation(o, i, F.Copy), rd, wr)

        def z_codes(h):
            a, b = PARTS[h]
            qz(zc[:, a:b], zs[:, a:b], zt[:, 4 * a:4 * b], ["zt%d.%d" % (i, h) for i in range(4)], "zc")

        for k in range(1, 8):
            kr, kn = keys[k % 2]
            k0, k1 = kn + ".0", kn + ".1"

            def pick(b, rd):
                scan(T.col[:, 96 * b:96 * b + 96], kr[:, 96 * b:96 * b + 96], T.k96[:, 96 * b:96 * b + 96], rd + ("k96",), "col%d" % b)

            def less(b, h):
                a, e = PARTS[h]
                ts(ct[:, 4 * a + b:4 * e:4], kr[:, a:e], -B96, T.col[:, 96 * b + 95:96 * b + 96], A.add, A.is_lt, ((k0, k1)[h], "col%d" % b), "ct%d.%d" % (b, h))

            grow(k - 1, 0)
            if k > 1: turns(1)
            pick(0, (k0,))
            grow(k - 1, 1)
            less(0, 0)
            pick(2, (k1,))
            for h, (a, b) in enumerate(PARTS):
                act(ct[:, 4 * a + 2:4 * b:4], kr[:, a:b], F.Sign, ((k0, k1)[h], "col2"), "ct2.%d" % h, bias=T.col[:, 287:288], scale=-1.0)
            pick(1, (k0, k1))
            less(0, 1)
            less(1, 0)
            less(1, 1)
            for h, (a, b) in enumerate(PARTS):
                qz(T.qt[:, a:b], T.qts[:, a:b], ct[:, 4 * a:4 * b], ["ct%d.%d" % (i, h) for i in range(3)] + ["ctz"], "qt%d" % h)
                mm((5, 1)[h], b - a, *kk(8), T.qt[:, a:b], T.qts[:, a:b], ("qt%d" % h, "kc8"))
            dx, dn = ((T.dd, "dd"), (T.de, "de"))[k % 2]
            dv = dx[:, 15:C:16]
            if t == 0:
                for i in {1: (11, 12), 2: (13, 14, 0), 3: (15, 16, 1), 4: (2, 3)}.get(k, ()):
                    kz(i)
            scan(dx[:, 0:H], ps(5, H), T.k16[:, 0:H], ("ps5", "k16"), dn + "0")
            if k <= 3:
                if t == 0:
                    table(2 * k)
                    table(2 * k + 1)
                elif k == 1:
                    table(6)
                    table(7)
                keep(2 * k)
                keep(2 * k + 1)
            if k in (4, 5):
                for b in (2 * k - 8, 2 * k - 7):
                    mm(fb[b], C, *kk(b), lc[:], ls[:], ln + ("kc%d" % b,))
                    act(T.ff[:, C * b:C * b + C], ps(fb[b]), F.Copy, "ps%d" % fb[b], "ff%d" % b)
            if k in (6, 7):
                for b in (2 * k - 12, 2 * k - 11):
                    op("s", lambda: S.activation(T.fs[:, C * b:C * b + C], T.ff[:, C * b:C * b + C].indirect(T.ow[:]), F.Copy), ("ff%d" % b, "ow"), "fs%d" % b)
            if k < 7: turns(0)
            else:
                for i in range(3):
                    z_list(0, i)
            scan(dx[:, H:C], ps(1, C - H), T.k16[:, H:C], ("ps1", "k16"), dn + "1")
            p0, m = 32 * (k // 2), k % 2
            p1 = p0 + 32
            nb, nn = ((T.ne, "ne"), (T.no, "no"))[m]
            if k < 7: act(nb[p0:p1, :], dv[p0:p1, :], F.Identity, (dn + "0", dn + "1", "mk"), nn, bias=T.mk[p0:p1, 2 + m:3 + m], scale=T.mk[p0:p1, m:m + 1])
        z_part(0, 0, True)
        z_part(3, 0, False)
        z_list(1, 0)
        z_part(1, 0, True)
        z_list(1, 1)
        z_part(2, 0, True)
        z_list(1, 2)
        z_codes(0)
        z_part(0, 1, True)
        z_part(2, 1, False)
        z_part(3, 1, False)
        z_part(1, 1, True)
        z_codes(1)
        if t:
            turns(0)
            turns(1)
        dv = T.dd[:, 15:C:16]
        for b in range(4):
            for h in range(2):
                w = 128 * (b + 4 * h)
                mm(2 * b + h, C, T.wk[:, w:w + 128], T.wp[:, w:w + 128], zc[:], zs[:], ("zc", "wk", "wp"))
        op("v", lambda: V.tensor_copy(T.nv[:].indirect(T.nz[:]), T.ij[:]), ("ij", "nz0", "nz1"), "nv")
        cp(T.kr[:], T.nv[:].indirect(T.aw[:]), ("nv", "aw"), "kr")
        if t:
            grow(7, 0)
            grow(7, 1)
        scan(T.dd[:], T.kr[:], T.k16[:], ("kr", "k16"), D01)
        ts(T.kw[:], dv, B16, None, A.add, None, D01, "kw")

        def largest(b):
            act(T.y1[:, C * b:C * b + C], ps(2 * b), F.Copy, "ps%d" % (2 * b), "y1%d" % b)
            tt(T.ym[:, C * b:C * b + C], ps(2 * b + 1), T.y1[:, C * b:C * b + C], A.max, ("ps%d" % (2 * b + 1), "y1%d" % b), "ym%d" % b)

        def put(b, v):
            o, i = T.yt[:, b:4 * C:4], T.ym[:, C * b:C * b + C].indirect(T.kw[:])
            rd, wr = ("ym%d" % b, "kw"), "yt%d" % b
            if v: op("v", lambda: V.tensor_scalar(o, i, 0.03125, None, A.mult), rd, wr)
            else: op("s", lambda: S.activation(o, i, F.Copy, scale=0.03125), rd, wr)

        for b in range(3):
            largest(b)
        put(0, True)
        largest(3)
        put(1, False)
        put(2, False)
        put(3, True)
        qn = ("qc%d" % t, "qs%d" % t)
        qz(T[qn[0]][:], T[qn[1]][:], T.yt[:], ["yt%d" % b for b in range(4)], qn)
        send(qn, ("bc%d" % t, "bs%d" % t), "ay%d" % t, peer)
        for b in range(4):
            mm(b, C, *kk(b), xc[:], xs[:], xn + ("kc%d" % b,), True, False)
        if t == 1:
            tt(T.to[0:1, :], T.key0[0:1, :], T.ij[0:1, :], A.add, ("key0.0", "key0.1", "ij"), "to")
            ts(T.to[0:1, :], T.to[0:1, :], 1.0 / 512, 1152.0, A.mult, A.add, "to", "to")
            ld("y", T.tot[:], T.to[0:1, :], "tot", "to")
            qz(T.vq[:], T.vs[:], T.vt[:], "vt", "vq")
        xt = T["xt%d" % (t + 1)]
        for b in range(4):
            mm(b, C, *kk(b), T["bc%d" % t][:], T["bs%d" % t][:], ("bc%d" % t, "bs%d" % t, "kc%d" % b), False, True)
        for b in range(4):
            if b % 2 == 0: act(xt[:, b:4 * C:4], ps(b), F.Copy, "ps%d" % b, "x%d" % b)
            else: cp(xt[:, b:4 * C:4], ps(b), "ps%d" % b, "x%d" % b)
        nx = ("xc%d" % (t + 1), "xs%d" % (t + 1))
        qz(T[nx[0]][:], T[nx[1]][:], xt[:], ["x%d" % b for b in range(4)], nx)
        if t == 0:
            send(nx, ("lc1", "ls1"), "ax1", peers[1])
    ld("y", T.oc[:], T.xc2[:].bitcast(dt.uint8), "oc", "xc2")
    for k in range(4):
        ld("s" if k % 2 else "y", T.osc[4 * k:4 * k + 4, :], T.xs2[32 * k:32 * k + 4, :], "osc%d" % k, "xs2")
    mm(4, C, T.vq[:], T.vs[:], T.xc2[:], T.xs2[:], ("xc2", "xs2", "vq"))
    act(T.yo[:], ps(4), F.Copy, "ps4", "yo")
    ld("s", T.y[:], T.yo[:], "yout", "yo")
    for q in "vstg":
        g.wait_ge(T.sem["c" + q], cnt[q])
    for i in range(ndma[0]):
        g.wait_ge(T.sem[DMAS[i]], 16)
    g.wait_ge(T.sem.sent, sent[0])
    for t in range(2):
        for s in ("ax", "ay"):
            g.wait_ge(T.sem[s + "%d" % t], 2 * len(topo.engines(core, peers[t])))
